import numpy as np, ml_dtypes
CORES = [16,18,20,22]
N = 4
BF = ml_dtypes.bfloat16
W, S, RO, LIM = 4096, 256, 4, 6
HEARER = [[1, 2, 3, 0], [2, 3, 0, 1], [3, 0, 1, 2], [1, 2, 3, 0]]
def world(rng, skew):
    m = rng.integers(2, 5, (8, 1, 1)); pn = rng.integers(2, 9, (1, 8, 1)); noise = 0.05 + 0.45 * rng.random((N, 8, 1, 1))
    alph = np.argsort(rng.random((8, 16, 513)), axis=-1)[..., :4] - 256
    proto = (rng.random((8, 8, 16)) * m).astype(np.int64); z = (rng.random((N, 8, W)) * pn).astype(np.int64)
    e = proto[np.arange(8)[None, :, None], z]
    u = (rng.random(e.shape, dtype=np.float32) ** skew * m).astype(np.int64)
    e = np.where(rng.random(e.shape, dtype=np.float32) < noise, np.minimum(u, 3), e)
    return np.ascontiguousarray(alph[np.arange(8)[None, :, None, None], np.arange(16), e].transpose(0, 1, 3, 2))
def parts(rng, skew=1):
    X = world(rng, skew)
    As = np.minimum((W * rng.random((N, 8, 16, W)) ** skew).astype(np.int64), W - 1)
    C = np.minimum((W * rng.random((N, 8, 16, S)) ** skew).astype(np.int64), W - 1); H = np.minimum((W * rng.random((N, 8, 16, S)) ** skew).astype(np.int64), W - 1)
    R = np.argsort(rng.random((N, 8, 16, S)), axis=2); A = np.minimum((256 * rng.random((N, 8, S)) ** skew).astype(np.int64), 255)
    return X, As, C, H, R, A
def pack(X, As, C, H, R, A):
    return {"x": np.ascontiguousarray(X.reshape(N, 128, W)).astype(np.float32).astype(BF), "assoc": np.ascontiguousarray(As.reshape(N, 128, W)).astype(np.int32),
            "ctx": np.ascontiguousarray(C.reshape(N, 128, S)).astype(np.int32), "cand": np.ascontiguousarray(H.reshape(N, 128, S)).astype(np.int32),
            "pref": np.ascontiguousarray(R.reshape(N, 128, S)).astype(np.int32), "fail0": np.ascontiguousarray(A).astype(np.int32)}
def setup_inputs(rng):
    return pack(*parts(rng))
def setup_inputs_spread(rng):
    X, As, C, H, R, A = parts(rng, 3)
    X = np.where((X == X[0, :, :, :1]) & (rng.random((8, 16, 1)) < 0.5), 0, X)
    share = 0.05 + 0.4 * rng.random((N, 8, 1, 1))
    X = np.where(rng.random((N, 8, 1, W)) < share, rng.integers(-256, 257, X.shape), X)
    X = np.where((X == 0) & (rng.random(X.shape, dtype=np.float32) < 0.5), -0.0, X)
    return pack(X, As, C, H, R, A)
def endlist(rng, shape):
    return np.where(rng.random(shape) < 0.68, rng.choice(np.array([0, W - 1]), shape), rng.integers(0, W, shape))
def setup_inputs_ends(rng):
    proto = rng.choice(np.array([-1, 1]), (8, 6, 16)); e = proto[np.arange(8)[None, :, None], rng.integers(0, 6, (N, 8, W))]
    e = np.where(rng.random(e.shape, dtype=np.float32) < 0.05 + 0.3 * rng.random((N, 8, 1, 1)), -e, e)
    u = rng.random((N, 8, W, 1)); e = np.where(u < 0.15, 1, np.where(u < 0.3, -1, e))
    X = np.ascontiguousarray(256 * e.transpose(0, 1, 3, 2)); sg = 256 * rng.choice(np.array([-1, 1]), (8, 1)); a = np.arange(16)[:, None]
    X[..., 0] = -sg; X[..., W - 1] = sg
    X[..., W - 16:W - 1] = sg[:, :, None] * np.where(np.arange(16)[:, None] == np.arange(1, 16), -1, 1)
    X[..., 1:16] = -X[..., W - 16:W - 1]
    X[..., 16:32] = sg[:, :, None] * np.where((a >= 1) & (a <= np.arange(16)), 1, -1)
    As = endlist(rng, (N, 8, 16, W)); C = endlist(rng, (N, 8, 16, S)); H = endlist(rng, (N, 8, 16, S))
    C[..., S - 8:] = np.concatenate([np.array([W - 1]), np.arange(W - 16, W - 1)])[:, None]
    H[..., S - 3:] = 0; H[:, :, 15, S - 1] = W - 1; H[:, :, 14:, S - 3] = W - 1
    C[..., S - 4] = a[:, 0]; H[..., S - 4] = W - 1
    H[..., S - 8:S - 4] = 31 - np.arange(11, 15) - (a < rng.integers(1, 16, (N, 8, 1, 4)))
    C[..., 0] = W - 1; C[:, :, 0, 0] = 0; H[..., 0] = W - 1
    C[..., 1] = W - 1; H[..., 1] = 0
    R = np.where(rng.random((N, 8, 1, S)) < 0.5, a, 15 - a); R = np.where(rng.random((N, 8, 1, S)) < 0.25, np.argsort(rng.random((N, 8, 16, S)), axis=2), R)
    return pack(X, As, C, H, R, rng.choice(np.array([0, 255]), (N, 8, S)))
def setup_inputs_corners(rng):
    X, As, C, H, R, A = parts(rng); k = np.arange(16); kk = k[:, None]; o = np.arange(1, S, 2); M = len(o); sp = np.argsort(np.array(HEARER[0]))
    A = rng.choice(np.array([0, 1, 2, 3, 252, 253, 254, 255]), (N, 8, S))
    R = np.where(rng.random((N, 8, 1, S)) < 0.3, np.where(rng.random((N, 8, 1, S)) < 0.5, kk, 15 - kk), R)
    rk = R[..., o].transpose(0, 1, 3, 2)[:, :, :, None, :]
    kind = rng.integers(0, 4, (N, 8, M, 1, 1)); b = rng.integers(-256, 256, (N, 8, M, 1, 16))
    one = (rk == kk) | ((rk > kk) & (rng.random((N, 8, M, 16, 16)) < 0.5))
    dx = (((kind == 1) & one) | (kind == 2) | ((kind == 3) & (rk == 15) & (kk >= 8))) & (kk > 0)
    room = (LIM + (A[..., o] & 3))[..., None, None]; how = rng.integers(0, 4, (N, 8, M, 1, 1))
    m = np.where(how == 0, 0, np.where(how == 1, room, np.where(how == 2, room + 1, 16)))
    w = np.where(kind == 0, 0, rng.choice(np.array([0, 1, 14, 15]), (N, 8, M, 1, 1)))
    dy = np.where(kind == 3, rk < m, rk >= 16 - m) | (kk < w)
    cols = (16 * o[:, None] + k).reshape(-1)
    X[..., cols] = (b + dx).transpose(0, 1, 4, 2, 3).reshape(N, 8, 16, 16 * M)
    X[..., cols - 16] = (b + dy).transpose(0, 1, 4, 2, 3).reshape(N, 8, 16, 16 * M)[sp]
    C[..., o] = 16 * o + kk; H[..., o] = 16 * (o - 1) + kk
    C[:, 6, :, 0::2] = C[:, 6, :1, 0::2]; H[:, 2, :, 0::2] = H[:, 2, :1, 0::2]
    As[:, 3] = np.where(rng.random((N, 16, W)) < 0.5, np.arange(W), As[:, 3]); As[:, 5] = rng.choice(np.array([0, W - 1]), (N, 16, W))
    return pack(X, As, C, H, R, A)
def setup_inputs_bulk(rng):
    X, As, C, H, R, A = parts(rng); h = W // 2; v = h // 2; m = min(LIM, 8)
    ga, gb, gc, gd, ge = [int(i) for i in rng.permutation(8)[:5]]
    X[:, ga, :, :h] = 2 * rng.integers(-128, 129, (N, 16, h)); X[:, gb, :, :h] = 2 * rng.integers(-128, 129, (16, 1))
    for g in (ga, gb):
        X[:, g, :, h:] = 2 * rng.integers(-128, 128, (N, 16, W - h)) + 1
        C[:, g] = rng.integers(h, W, (N, 16, S)); C[:, g, 0] = rng.integers(0, h, (N, S))
    H[:, ga] = rng.integers(h, W, (N, 16, S)); H[:, gb] = rng.integers(0, h, (N, 16, S))
    X[:, gc] = (np.argsort(rng.random((16, 513)), axis=-1)[:, :N] - 256).T[:, :, None]; A[:, gc, ::2] = 255
    X[:, gd] = 2 * rng.integers(-128, 128, (16, 1))
    X[:, gd, 8:8 + m, v:h] += rng.integers(0, 2, (N, m, h - v)); X[:, gd, :8, h:] += rng.integers(0, 2, (N, 8, W - h))
    C[:, gd] = rng.integers(h, W, (N, 16, S)); C[:, gd, 0] = rng.integers(0, v, (N, S)); H[:, gd] = rng.integers(v, h, (N, 16, S))
    near = LIM + ((254 + RO) & 3); b = 2 * rng.integers(-128, 128, (16, 1))
    X[:, ge, :, :h] = b; X[:, ge, :, h:] = b + 1; X[:, ge, :, h + v:] = b + (np.argsort(rng.random(16)) < near)[:, None]; X[:, ge, :, ::16] = b
    C[:, ge] = h + 2 * rng.integers(0, v // 2, (N, 16, S)) + 1
    H[:, ge] = N * rng.integers(0, h // N, (N, 16, S)) + np.arange(N)[:, None, None]
    As[:, ge, 0, :h] = h + v * (np.arange(h) % N == np.array(HEARER[RO - 2])[:, None]) + 2 * rng.integers(0, v // 2, (N, h)) + 1
    A[:, ge, ::2] = 255
    return pack(X, As, C, H, R, A)
def check_inputs(d):
    bad = []
    for name, lo, hi in (("x", -256, 256), ("assoc", 0, W - 1), ("ctx", 0, W - 1), ("cand", 0, W - 1), ("pref", 0, 15), ("fail0", 0, 255)):
        v = np.asarray(d[name]).astype(np.float64)
        if not (np.min(v) >= lo and np.max(v) <= hi): bad.append("range of " + name)
        if np.any(v != np.rint(v)): bad.append("whole numbers in " + name)
    if np.any(np.sort(np.asarray(d["pref"]).astype(np.int64).reshape(-1, 8, 16, S), axis=2) != np.arange(16)[:, None]): bad.append("permutations in pref")
    return bad
def pick(a, ix):
    return np.take_along_axis(a, ix.reshape(N, 8, 1, 16 * S), 3).reshape(N, 8, 16, 16, S)
def front(R, row, fail):
    old = np.take_along_axis(R, row[:, :, None, :], 2)
    moved = np.where(np.arange(16)[:, None] == row[:, :, None, :], 0, R + (R < old))
    return np.where(fail[:, :, None, :], moved, R)
def reference(x, assoc, ctx, cand, pref, fail0):
    X = x.astype(np.float32).astype(np.int16).reshape(N, 8, 16, W); As = assoc.astype(np.int64).reshape(N, 8, 16, W)
    C = ctx.astype(np.int64).reshape(N, 8, 16, S); H = cand.astype(np.int64).reshape(N, 8, 16, S); R = pref.astype(np.int64).reshape(N, 8, 16, S); A = fail0.astype(np.int64).reshape(N, 8, S)
    for t in range(RO):
        q = np.array(HEARER[t]); sp = np.argsort(q)
        xk = pick(X, C); x0 = xk[:, :, :, 0]
        first = np.min(np.where(xk != x0[:, :, :, None], R[:, :, :, None], 16), axis=2)
        desc = np.any(R[:, :, :, None] == first[:, :, None], axis=3)
        top = np.min(first, axis=2)
        yk = pick(X, H)[q]
        miss = np.sum((yk != x0[:, :, :, None]) & desc[:, :, :, None], axis=2)
        ks = np.argmin(miss, axis=2)
        n = np.take_along_axis(H[q], ks[:, :, None, :], 2)[:, :, 0]
        y = np.take_along_axis(yk, ks[:, :, None, None, :], 3)[:, :, :, 0]
        un = y != x0; fail = np.sum(un, axis=2) > LIM + (A & 3); row = np.argmin(np.where(un, R, 16), axis=2)
        A = A + fail
        R = front(R, row, fail); R = front(R, row[sp], fail[sp])
        cn = np.take_along_axis(As, n[:, :, None, :], 3); hn = np.take_along_axis(As, n[sp][:, :, None, :], 3)
        C = np.where((first == top[:, :, None]) & (first < 16), cn, C); C[:, :, 0] = cn[:, :, 0]
        H = np.where(miss[sp] > 0, hn, H)
        if t < RO - 1:
            put = np.broadcast_to((16 * np.arange(S) + ks[sp])[:, :, None, :], (N, 8, 16, S))
            np.put_along_axis(X, put, np.where(desc, x0, y)[sp], 3)
    return {"yctx": C.reshape(N, 128, S).astype(np.float32), "ycand": H.reshape(N, 128, S).astype(np.float32), "ypref": R.reshape(N, 128, S).astype(np.float32), "yfail": A.astype(np.float32)}

@@ -1,0 +1,616 @@
+import math
+from concourse.mybir import AluOpType as OP, ActivationFunctionType as AF
+
+N = 4
+DIST = [1, 2, 3, 1]
+RO = len(DIST)
+S = 256
+W = 4096
+NH = 2
+HS = S // NH
+LN2 = math.log(2.0)
+WT = 85
+CFG = {"npc": 4,
+       "vc": ((0, 3),),
+       "vh": (),
+       "ns": 5,
+       "es": 1,
+       "bitV": True, "dbV": True, "alpha": 20.0, "win": 300.0,
+       "bonus": 1500.0, "g": 1.5, "f": 1.22, "ov": 12.0, "wake": 80.0, "hop": 2000.0}
+
+SCRATCH = {}
+for _n, _s, _d in [
+    ("X", [128, W], "bfloat16"), ("ASI", [128, W], "int32"), ("ASH", [128, W], "float32"),
+    ("XG", [128, W], "bfloat16"), ("YG", [128, W], "bfloat16"), ("DW", [128, W], "bfloat16"), ("E", [128, W], "bfloat16"), ("G", [128, W], "bfloat16"),
+    ("CIN", [128, S], "int32"), ("HIN", [128, S], "int32"), ("RIN", [128, S], "int32"), ("FIN", [8, S], "int32"), ("Q8I", [8, S], "int32"),
+    ("A8", [8, S], "bfloat16"), ("Q8", [8, S], "bfloat16"), ("AB", [128, S], "bfloat16"), ("Q0", [128, S], "bfloat16"), ("IND", [128, S], "bfloat16"),
+    ("C", [128, S], "float32"), ("C16", [128, S], "uint16"), ("HK", [128, S], "float32"), ("H16", [128, S], "uint16"),
+    ("R", [128, S], "bfloat16"), ("R1", [128, S], "bfloat16"), ("MA", [128, S], "bfloat16"), ("LA", [128, S], "bfloat16"), ("IW", [128, S], "bfloat16"),
+    ("AB1", [128, S], "bfloat16"), ("BIT", [128, S], "bfloat16"), ("TI", [128, S], "int32"), ("SG", [128, S], "bfloat16"), ("KAP", [128, S], "bfloat16"),
+    ("CM", [128, S], "float32"), ("KH", [128, S], "float32"), ("HM", [128, S], "float32"), ("UND", [128, S], "bfloat16"), ("DSC", [128, S], "bfloat16"),
+    ("XD", [128, S], "bfloat16"), ("YU", [128, S], "bfloat16"), ("KT", [128, S], "float32"), ("SC", [128, S], "float32"),
+    ("K32", [128, 16], "int32"), ("N32", [128, 16], "int32"), ("KK", [128, 16], "int32"), ("OF", [128, 16], "int32"), ("OF16", [128, 16], "uint16"),
+    ("DM", [128, S], "bfloat16"), ("DMW", [128, S], "bfloat16"), ("TH", [128, S], "float32"),
+    ("OC", [128, S], "float32"), ("OH", [128, S], "float32"), ("OR", [128, S], "float32"), ("OA", [128, S], "float32"),
+    ("IP", [128, 1], "int32"), ("KI", [128, 1], "int32"), ("B4I", [128, 1], "int32"), ("COL", [128, 16], "float32"), ("COL2", [128, 2], "float32"), ("EA", [128, 1024], "bfloat16"), ("COLB", [128, 2], "bfloat16"),
+    ("IM", [128, 128], "float32"), ("IMG", [128, 128], "float32"), ("IMK", [128, 128], "float32"), ("JS", [128, 2048], "bfloat16"),
+    ("SEL", [128, 2048], "bfloat16"), ("CNT", [128, 2048], "bfloat16"),
+    ("mB", [128, 128], "bfloat16"), ("mI", [128, 128], "bfloat16"), ("mNI", [128, 128], "bfloat16"), ("mNB", [128, 128], "bfloat16"),
+    ("mTB", [128, 128], "bfloat16"), ("mWB", [128, 128], "bfloat16"), ("mCW", [128, 128], "bfloat16"), ("mKC", [128, 128], "bfloat16"),
+    ("mHF", [128, 128], "bfloat16"), ("ONES", [128, 128], "bfloat16"), ("mI2", [128, 128], "bfloat16"), ("TMP", [128, 128], "float32"), ("MK0", [128, 128], "float32"),
+    ("fI", [128, 128], "float32"), ("fP", [128, 512], "float32"), ("SD", [128, 128], "float32"), ("CII", [128, 16], "int32"), ("CI", [128, 16], "int32"),
+    ("mG8", [8, 128], "bfloat16"),
+]:
+    SCRATCH[_n] = ("sbuf", _s, _d)
+for _t in range(RO):
+    SCRATCH["M0_%d" % _t] = ("sbuf", [128, 3 * S], "bfloat16")
+    SCRATCH["L0_%d" % _t] = ("sbuf", [128, 3 * S], "bfloat16")
+    for _n in ("M1_", "L1_", "FF_", "LF_"):
+        SCRATCH[_n + str(_t)] = ("sbuf", [128, S], "bfloat16")
+    for _n in ("NS_", "LN_"):
+        SCRATCH[_n + str(_t)] = ("sbuf", [128, 16], "uint16")
+for _b in range(8):
+    SCRATCH["pb%d" % _b] = ("psum", [128, 512], "float32")
+
+SEMAPHORES = ["sT", "sV", "sS", "sG"]
+SEMAPHORES += ["ld_%s" % _n for _n in ("x", "ctx", "cand", "pref", "assoc", "fail0")] + ["st_%d" % _i for _i in range(12)]
+for _t in range(RO):
+    for _m in ("00", "01", "10", "11", "20", "21", "30", "31"):
+        SEMAPHORES += ["r%d_%s" % (_t, _m), "l%d_%s" % (_t, _m)]
+
+cP, cK, cG16, cPp, cPm, cS0, cS1, cKC, c16K, cH, c16P = range(11)
+
+_ORDER = {}
+
+
+PER_ROUND = ("L10", "L11", "L00", "L01", "NS0", "NS1", "LN0", "LN1", "x0_0", "x0_1", "x0p0", "x0p1")
+
+
+def build(g, T, topo, rank, core):
+    ops = []
+    cur_t = [0]
+    cur_h = [0]
+    GR = CFG["g"]
+
+    def key(k):
+        return k + "_r%d" % cur_t[0] if k in PER_ROUND else k
+
+    def add(q, fn, rd, wr, cost, banks=(), sem=None, val=1, lat=0.0):
+        ops.append({"q": q, "fn": fn, "rd": [key(k) for k in rd], "wr": [key(k) for k in wr], "bk": list(banks), "cost": cost, "sem": sem, "val": val, "lat": lat,
+                    "h": cur_h[0], "t": cur_t[0]})
+
+    CY = 0.83 * CFG["f"]
+
+    def vcost(n, rate=1.0):
+        return max(64, n * rate) * CY + CFG["ov"]
+
+    def V(name, rd, wr, n, rate=1.0, banks=(), extra=0.0, **kw):
+        f = {"tt": g.vector.tensor_tensor, "ts": g.vector.tensor_scalar, "cp": g.vector.tensor_copy, "tr": g.vector.transpose,
+             "scan": g.vector.tensor_tensor_scan}[name]
+        add("V", lambda: f(**kw), rd, wr, vcost(n, rate) + extra, banks)
+
+    def A(rd, wr, n, banks=(), extra=0.0, rate=1.0, **kw):
+        add("S", lambda: g.scalar.activation(**kw), rd, wr, n * rate * CY + 20 + extra, banks)
+
+    def MM(lst, rd, wr, banks):
+        def fn():
+            ins = None
+            for o, l, r, a, b, n, f in lst:
+                ins = g.tensor.matmul(out=o, lhsT=l, rhs=r, start=a, stop=b)
+            return ins
+        add("T", fn, rd, wr, sum(max(64, n) * (4 if f else 1) * 0.42 * 1.22 for o, l, r, a, b, n, f in lst) + 20, banks)
+
+    def col(i):
+        return T.COL[:, i:i + 1]
+
+    def sl(b, h):
+        return b[:, h * HS:(h + 1) * HS]
+
+    def m0(b, h, j):
+        return b[:, (3 * h + j) * HS:(3 * h + j + 1) * HS]
+
+    def ps(b, r):
+        return T["pb%d" % b][:, r * 128:(r + 1) * 128]
+
+    def ldw(q, semn, key, dst, src, lat):
+        e = g.sync if q == "Y" else g.scalar
+        add(q, lambda: e.dma_start(out=dst, in_=src), [], [key], 60, sem="ld_" + semn, val=16, lat=lat)
+
+    ldw("Y", "ctx", "CIN", T.CIN[:], T.ctx[:], 2200)
+    ldw("S", "x", "X", T.X[:], T.x[:], 4500)
+    ldw("Y", "pref", "RIN", T.RIN[:], T.pref[:], 2300)
+    ldw("Y", "cand", "HIN", T.HIN[:], T.cand[:], 2400)
+    ldw("Y", "fail0", "FIN", T.FIN[:], T.fail0[:], 2400)
+    ldw("S", "assoc", "ASI", T.ASI[:], T.assoc[:], 8500)
+
+    def iota(dst, key, pattern, base, cm, n, flag=True):
+        if flag:
+            fn = lambda: g.iota(dst, pattern, base, cm, allow_small_or_imprecise_dtypes=True)
+        else:
+            fn = lambda: g.iota(dst, pattern, base, cm)
+        add("G", fn, [], [key], 130 + 2 * n * CY)
+
+    iota(T.IP[:], "IP", [[1, 1]], 0, 1, 1, False)
+    iota(T.IM[:], "IM", [[1, 128]], 0, 0, 128)
+    iota(T.IMG[:], "IMG", [[16, 8], [0, 16]], 0, 0, 128)
+    iota(T.JS[:], "JS", [[-1, 16], [1, 128]], 0, 0, 2048)
+    iota(T.IMK[:], "IMK", [[0, 8], [1, 16]], 0, 0, 128)
+    iota(T.CII[:], "CII", [[256, 16]], 15, 0, 16, False)
+
+    V("cp", ["CIN"], ["C160", "C161"], S, out=T.C16[:], in_=T.CIN[:])
+
+    V("ts", ["IP"], ["KI"], 1, out=T.KI[:], in0=T.IP[:], scalar1=15, scalar2=None, op0=OP.bitwise_and)
+    V("cp", ["IP"], ["cP"], 1, out=col(cP), in_=T.IP[:])
+    V("cp", ["KI"], ["cK"], 1, out=col(cK), in_=T.KI[:])
+    V("tt", ["cP", "cK"], ["cG16"], 1, out=col(cG16), in0=col(cP), in1=col(cK), op=OP.subtract)
+
+    def mat(dst, key, src, skey, c, ckey, n=128, rate=1.0):
+        V("ts", [skey, ckey], [key], n, rate, out=dst, in0=src, scalar1=c, scalar2=None, op0=OP.is_equal)
+
+    mat(T.mI[:], "mI", T.IM[:], "IM", col(cP), "cP")
+    V("ts", ["mI"], ["mNI"], 128, 0.5, out=T.mNI[:], in0=T.mI[:], scalar1=-1.0, scalar2=None, op0=OP.mult)
+
+    def scol(i, key, src, skey, **kw):
+        V("ts", [skey], [key], 1, out=col(i), in0=src, **kw)
+
+    def state_from_pref():
+        V("cp", ["RIN"], ["R0", "R1_"], S, out=T.R[:], in_=T.RIN[:])
+    state_from_pref()
+    ops[-1]["wr"] = ["Rs0", "Rs1"]
+
+    def orders(h, t, src, rd, banks=()):
+        A(rd, ["w%d_%d" % (t, h)], HS, banks, out=m0(T["M0_%d" % t], h, 1), in_=src, func=AF.Exp, bias=col(12), scale=-11.0 * LN2)
+        ops[-1]["rd"].append("bias")
+        A(rd + ["bias"], ["IW%d" % h], HS, banks, out=sl(T.IW, h), in_=src, func=AF.Exp, bias=col(13), scale=LN2)
+
+    add("V", lambda: g.vector.memset(col(12), WT * LN2), [], ["bias"], 80)
+    add("V", lambda: g.vector.memset(col(13), -16.0 * LN2), [], ["bias"], 80)
+    add("V", lambda: g.vector.memset(col(14), 15.0 * LN2), [], ["bias"], 80)
+    for h in range(NH):
+        orders(h, 0, sl(T.R, h), ["Rs%d" % h])
+
+    mat(T.SEL[:], "SEL", T.JS[:], "JS", col(cG16), "cG16", 2048, 0.5)
+    for j in range(4):
+        MM([(T["pb%d" % j][:, 0:512], T.mI[:], T.SEL[:, j * 512:(j + 1) * 512], True, True, 512, False)], ["mI", "SEL"], ["ring%d" % j], [j])
+        m = 512 if j < 3 else 384
+        V("tt", ["SEL", "ring%d" % j], ["CNT"], m, 1.0, [j], out=T.CNT[:, j * 512:j * 512 + m], in0=T["pb%d" % j][:, 0:m], in1=T.SEL[:, j * 512 + 128:j * 512 + 128 + m], op=OP.subtract)
+    V("cp", ["SEL"], ["CNT"], 128, 0.5, out=T.CNT[:, 1920:2048], in_=T.SEL[:, 1920:2048])
+    ns = CFG["ns"]
+    if ns:
+        V("ts", ["CNT"], ["CNT"], 128 * ns, 0.5, out=T.CNT[:, 0:128 * ns], in0=T.CNT[:, 0:128 * ns], scalar1=0.5, scalar2=None, op0=OP.mult)
+        V("ts", ["cK"], ["c8a"], 1, out=T.COL2[:, 0:1], in0=col(cK), scalar1=0.0, scalar2=8.0, op0=OP.is_equal, op1=OP.mult)
+        V("ts", ["cK"], ["c8b"], 1, out=T.COL2[:, 1:2], in0=col(cK), scalar1=float(ns), scalar2=8.0, op0=OP.is_equal, op1=OP.mult)
+        V("tt", ["c8a", "c8b"], ["c8"], 1, out=col(15), in0=T.COL2[:, 0:1], in1=T.COL2[:, 1:2], op=OP.subtract)
+    else:
+        add("V", lambda: g.vector.memset(col(15), 0.0), [], ["c8"], 80)
+    mat(T.mB[:], "mB", T.IMG[:], "IMG", col(cG16), "cG16")
+    add("V", lambda: g.vector.memset(T.ONES[:], 1.0), [], ["ONES"], 80)
+    A(["cK", "bias"], ["cb2"], 1, out=T.COLB[:, 0:1], in_=col(cK), func=AF.Exp, bias=col(14), scale=-LN2)
+    A(["cK", "bias"], ["cbw"], 1, out=T.COLB[:, 1:2], in_=col(cK), func=AF.Exp, bias=col(12), scale=-11.0 * LN2)
+    V("ts", ["mB", "cb2"], ["mWB"], 128, 1.0, out=T.mWB[:], in0=T.mB[:], scalar1=T.COLB[:, 0:1], scalar2=None, op0=OP.mult)
+    V("ts", ["mI"], ["mHF"], 128, 0.5, out=T.mHF[:], in0=T.mI[:], scalar1=0.5, scalar2=None, op0=OP.mult)
+    V("cp", ["HIN"], ["H160", "H161"], S, out=T.H16[:], in_=T.HIN[:])
+    V("ts", ["mB", "cbw"], ["TMP"], 128, 1.0, out=T.TMP[:], in0=T.mB[:], scalar1=T.COLB[:, 1:2], scalar2=-0.6, op0=OP.mult, op1=OP.mult)
+    V("ts", ["IMK"], ["MK0"], 128, 1.0, out=T.MK0[:], in0=T.IMK[:], scalar1=0.5, scalar2=None, op0=OP.is_gt)
+    V("tt", ["TMP", "MK0"], ["mCW"], 128, 2.0, out=T.mCW[:], in0=T.TMP[:], in1=T.MK0[:], op=OP.mult)
+    scol(cKC, "cKC", col(cK), "cK", scalar1=0.0, scalar2=-(2.0 ** -90), op0=OP.is_equal, op1=OP.add)
+    V("ts", ["mI", "cKC"], ["mKC"], 128, 1.0, out=T.mKC[:], in0=T.mI[:], scalar1=col(cKC), scalar2=None, op0=OP.mult)
+    mat(T.fI[:], "fI", T.IM[:], "IM", col(cP), "cP")
+    V("cp", ["CIN"], ["Cs0", "Cs1"], S, out=T.C[:], in_=T.CIN[:])
+    scol(cH, "cH", col(cK), "cK", scalar1=-4096.0, scalar2=61440.0, op0=OP.mult, op1=OP.add)
+    V("ts", ["HIN", "cH"], ["HK0", "HK1"], S, out=T.HK[:], in0=T.HIN[:], scalar1=col(cH), scalar2=2.0 ** -17, op0=OP.add, op1=OP.mult)
+    V("ts", ["mB"], ["mNB"], 128, 0.5, out=T.mNB[:], in0=T.mB[:], scalar1=-1.0, scalar2=None, op0=OP.mult)
+    V("ts", ["mI"], ["mI2"], 128, 0.5, out=T.mI2[:], in0=T.mI[:], scalar1=2.0, scalar2=None, op0=OP.mult)
+    V("tt", ["mI2", "mB"], ["mTB"], 128, 2.0, out=T.mTB[:], in0=T.mI2[:], in1=T.mB[:], op=OP.subtract)
+    V("ts", ["IP"], ["B4I"], 1, out=T.B4I[:], in0=T.IP[:], scalar1=4, scalar2=1, op0=OP.arith_shift_right, op1=OP.bitwise_and)
+    V("cp", ["B4I"], ["cS1"], 1, out=col(cS1), in_=T.B4I[:])
+    scol(cS0, "cS0", col(cS1), "cS1", scalar1=-1.0, scalar2=1.0, op0=OP.mult, op1=OP.add)
+    scol(cPp, "cPp", col(cP), "cP", scalar1=16.0, scalar2=None, op0=OP.add)
+    scol(cPm, "cPm", col(cP), "cP", scalar1=-16.0, scalar2=None, op0=OP.add)
+    scol(c16K, "c16K", col(cK), "cK", scalar1=16.0, scalar2=None, op0=OP.mult)
+    scol(c16P, "c16P", col(cP), "cP", scalar1=16.0, scalar2=None, op0=OP.mult)
+    for j, (c, ck, s, sk) in enumerate([(cP, "cP", cS0, "cS0"), (cPp, "cPp", cS0, "cS0"), (cPm, "cPm", cS1, "cS1"), (cP, "cP", cS1, "cS1")]):
+        V("ts", ["IM", ck, sk], ["fP"], 128, 1.0, out=T.fP[:, j * 128:(j + 1) * 128], in0=T.IM[:], scalar1=col(c), scalar2=col(s), op0=OP.is_equal, op1=OP.mult)
+    V("ts", ["IMK"], ["SD"], 128, 1.0, out=T.SD[:], in0=T.IMK[:], scalar1=0.0, scalar2=-4096.0, op0=OP.is_equal, op1=OP.mult)
+    V("ts", ["CII", "c16K"], ["CI"], 16, 1.0, out=T.CI[:], in0=T.CII[:], scalar1=col(c16K), scalar2=None, op0=OP.add)
+    V("ts", ["IMG", "c16P"], ["mG8"], 128, 1.0, out=T.mG8[:], in0=T.IMG[0:8, :], scalar1=T.COL[0:8, c16P:c16P + 1], scalar2=None, op0=OP.is_equal)
+    V("cp", ["FIN"], ["A8"], S, out=T.A8[:], in_=T.FIN[:])
+    V("ts", ["FIN"], ["Q8I"], S, out=T.Q8I[:], in0=T.FIN[:], scalar1=3, scalar2=None, op0=OP.bitwise_and)
+    V("cp", ["Q8I"], ["Q8"], S, out=T.Q8[:], in_=T.Q8I[:])
+    MM([(T.pb6[:, 0:256], T.mG8[:], T.A8[:], True, True, S, False), (T.pb6[:, 256:512], T.mG8[:], T.Q8[:], True, True, S, False)],
+       ["mG8", "A8", "Q8"], ["b6a"], [6])
+    A(["b6a"], ["AB"], S, [6], out=T.AB[:], in_=T.pb6[:, 0:256], func=AF.Copy)
+    A(["b6a"], ["Q0"], S, [6], out=T.Q0[:], in_=T.pb6[:, 256:512], func=AF.Copy)
+    for h in range(NH):
+        A(["Q0"], ["th0_%d" % h], HS, out=m0(T.M0_0, h, 2), in_=sl(T.Q0, h), func=AF.Copy, bias=6.5)
+    for j in range(8):
+        V("ts", ["ASI", "cH"], ["ASH"], W // 8, 1.0, out=T.ASH[:, j * 512:(j + 1) * 512], in0=T.ASI[:, j * 512:(j + 1) * 512],
+          scalar1=col(cH), scalar2=2.0 ** -17, op0=OP.add, op1=OP.mult)
+
+    def send(t, m, dst, src_ap, dst_ap, rd, wr, lat):
+        rid, pid, _s = topo.addr(dst)
+        mask = topo.mask(core, dst)
+        ne = len(topo.engines(core, dst))
+        rs, ls = "r%d_%s" % (t, m), "l%d_%s" % (t, m)
+        add("G", lambda: g.remote_dma(out_ap=dst_ap, in_ap=src_ap, remote_sem=T.sem[rs], local_sem=T.sem[ls], pid=pid, routing_id=rid, dma_engine_mask=mask),
+            rd, [], 700)
+        ops[-1]["remote"] = (ls, ne)
+        k = len(ops) - 1
+        add("N", None, [], wr, 0, sem=rs, val=ne, lat=lat)
+        ops[-1]["after"] = k
+
+    def gather(t, h, src16, dst, key, okey, vp):
+        npc = CFG["npc"]
+        step = HS // npc
+        for j in range(npc):
+            a = h * HS + j * step
+            offs = src16[:, a:a + step]
+            o = dst[:, 16 * a:16 * (a + step)]
+            n = 16 * step
+            if (h, j) in vp:
+                V("cp", ["X", okey + str(h)], [key + "%d%d" % (h, j)], n, GR, out=o, in_=T.X[:].indirect(offs))
+            else:
+                A(["X", okey + str(h)], [key + "%d%d" % (h, j)], n, (), 45, GR, out=o, in_=T.X[:].indirect(offs), func=AF.Copy)
+
+    ring = [0]
+
+    for t in range(RO):
+        hear = T.cores[(rank + DIST[t]) % N]
+        spk = T.cores[(rank - DIST[t]) % N]
+        M0, L0 = T["M0_%d" % t], T["L0_%d" % t]
+        M1, L1 = T["M1_%d" % t], T["L1_%d" % t]
+        NS, LN = T["NS_%d" % t], T["LN_%d" % t]
+        FF, LF = T["FF_%d" % t], T["LF_%d" % t]
+        last = t == RO - 1
+        cur_t[0] = t
+        for h in range(NH):
+            hs = str(h)
+            cur_h[0] = h
+            gather(t, h, T.C16, T.XG, "XG", "C16", CFG["vc"])
+            xgk = ["XG%d%d" % (h, j) for j in range(CFG["npc"])]
+
+            def xg(k, h=h):
+                return T.XG[:, h * 2048 + k:(h + 1) * 2048:16]
+            b4 = 4 + h
+            V("cp", xgk, ["x0_%d" % h], HS, 0.5, out=m0(M0, h, 0), in_=xg(0))
+            for c in range(4):
+                ks = range(1 + 4 * c, min(16, 5 + 4 * c))
+                b = ring[0] % 4
+                ring[0] += 1
+                lst = []
+                for j, k in enumerate(ks):
+                    lst.append((ps(b, j), T.mI[:], xg(k), True, False, HS, False))
+                    lst.append((ps(b, j), T.mNI[:], xg(0), False, True, HS, False))
+                MM(lst, xgk + ["mI", "mNI"], ["ring%d" % b], [b])
+                for j, k in enumerate(ks):
+                    V("tt", ["ring%d" % b, "w%d_%d" % (t, h)], ["DW%d_%d" % (h, k)], HS, 1.0, [b],
+                      out=T.DW[:, h * 2048 + k * 128:h * 2048 + (k + 1) * 128], in0=ps(b, j), in1=m0(M0, h, 1), op=OP.mult)
+                MM([(ps(b4, 0), T.SEL[:, k * 128:(k + 1) * 128], T.DW[:, h * 2048 + k * 128:h * 2048 + (k + 1) * 128], k == 1, k == 15, HS, False) for k in ks],
+                   ["SEL"] + ["DW%d_%d" % (h, k) for k in ks], ["Sk" + hs], [b4])
+            A(["Sk" + hs], ["ABS" + hs], HS, [b4], out=sl(T.AB1, h), in_=ps(b4, 0), func=AF.Abs)
+
+            def G(r, h=h):
+                return T.G[:, h * 2048 + r * 128:h * 2048 + (r + 1) * 128]
+            for r in range(16):
+                if r < CFG["ns"]:
+                    A(["ABS" + hs], ["G%d_%d" % (h, r)], HS, out=G(r), in_=sl(T.AB1, h), func=AF.Sign, scale=2.0 ** (11 * r - WT) / 0.6, bias=-1.0)
+                else:
+                    V("ts", ["ABS" + hs], ["G%d_%d" % (h, r)], HS, 0.5, out=G(r), in0=sl(T.AB1, h), scalar1=0.6 * 2.0 ** (WT - 11 * r), scalar2=None, op0=OP.is_ge)
+                if r % 4 == 3:
+                    MM([(ps(b4, 1), T.CNT[:, q * 128:(q + 1) * 128], G(q), q == 0, q == 15, HS, False) for q in range(r - 3, r + 1)],
+                       ["CNT"] + ["G%d_%d" % (h, q) for q in range(r - 3, r + 1)], ["cnt" + hs], [b4])
+            if CFG["bitV"]:
+                V("ts", ["cnt" + hs, "c8"], ["BIT" + hs], HS, 1.0, [b4], out=sl(T.BIT, h), in0=ps(b4, 1), scalar1=col(15), scalar2=0.5, op0=OP.add, op1=OP.is_gt)
+            else:
+                A(["cnt" + hs, "c8"], ["BIT" + hs], HS, [b4], out=sl(T.BIT, h), in_=ps(b4, 1), func=AF.Sign, bias=col(15))
+            MM([(ps(b4, 0), T.mHF[:], T.ONES[:], True, False, HS, False), (ps(b4, 0), T.mWB[:], sl(T.BIT, h), False, True, HS, False)],
+               ["mHF", "mWB", "ONES", "BIT" + hs], ["Sk" + hs], [b4])
+            V("tt", ["Sk" + hs, "IW" + hs], ["t2" + hs], HS, 1.0, [b4], out=ps(b4, 3), in0=ps(b4, 0), in1=sl(T.IW, h), op=OP.mult)
+            V("cp", ["t2" + hs], ["TI" + hs], HS, 1.0, [b4], out=sl(T.TI, h), in_=ps(b4, 3))
+            V("tt", ["t2" + hs, "TI" + hs], ["q" + hs], HS, 1.0, [b4], out=ps(b4, 2), in0=ps(b4, 3), in1=sl(T.TI, h), op=OP.subtract)
+            if CFG["dbV"]:
+                V("ts", ["q" + hs], ["dB" + hs], HS, 1.0, [b4], out=ps(b4, 1), in0=ps(b4, 2), scalar1=2.0 ** 28, scalar2=None, op0=OP.mult)
+            else:
+                A(["q" + hs], ["dB" + hs], HS, [b4], out=ps(b4, 1), in_=ps(b4, 2), func=AF.Copy, scale=2.0 ** 28)
+            ops[-1]["wr"].append("cnt" + hs)
+            V("tt", ["dB" + hs, "x0_%d" % h], ["x0p%d" % h], HS, 1.0, [b4], out=sl(M1, h), in0=ps(b4, 1), in1=m0(M0, h, 0), op=OP.max)
+            send(t, "1%d" % h, hear, sl(M1, h), sl(L1, h), ["x0p%d" % h], ["L1" + hs], 2000)
+            MM([(ps(b4, 1), T.mI[:], sl(T.AB1, h), True, False, HS, False), (ps(b4, 1), T.mCW[:], sl(T.BIT, h), False, False, HS, False),
+                (ps(b4, 1), T.mKC[:], T.ONES[:], False, True, HS, False)], ["ABS" + hs, "mI", "mCW", "mKC", "ONES", "BIT" + hs], ["cnt" + hs, "dB" + hs], [b4])
+            A(["cnt" + hs], ["SG" + hs], HS, [b4], out=sl(T.SG, h), in_=ps(b4, 1), func=AF.Sign)
+            A(["SG" + hs], ["KAP" + hs], HS, out=sl(T.KAP, h), in_=sl(T.SG, h), func=AF.Relu, scale=8192.0)
+            MM([(ps(b4, 2), T.fI[:], sl(T.C, h), True, False, HS, True), (ps(b4, 2), T.mNI[:], sl(T.KAP, h), False, True, HS, False)],
+               ["fI", "mNI", "Cs" + hs, "KAP" + hs], ["q" + hs], [b4])
+            send(t, "0%d" % h, hear, M0[:, h * 3 * HS:(h + 1) * 3 * HS], L0[:, h * 3 * HS:(h + 1) * 3 * HS], ["x0_" + hs, "w%d_%d" % (t, h), "th%d_%d" % (t, h)], ["L0" + hs], CFG["hop"] + 200)
+        for h in range(NH):
+            cur_h[0] = h
+            gather(t, h, T.H16, T.YG, "YG", "H16", CFG["vh"])
+        for h in range(NH):
+            hs = str(h)
+            cur_h[0] = h
+            ygk = ["YG%d%d" % (h, j) for j in range(CFG["npc"])]
+            b6 = 6 + h
+            V("ts", ["L1" + hs], ["DSC" + hs], HS, 0.5, out=sl(T.DSC, h), in0=sl(L1, h), scalar1=1000.0, scalar2=None, op0=OP.is_lt)
+            lst = [(ps(b6, 3), T.mI[:], m0(L0, h, 1), True, True, HS, False)]
+            if not last:
+                lst.append((ps(b6, 2), T.mI[:], sl(L1, h), True, True, HS, False))
+                V("ts", ["L1" + hs], ["UND" + hs], HS, 0.5, out=sl(T.UND, h), in0=sl(L1, h), scalar1=1000.0, scalar2=None, op0=OP.is_gt)
+            MM(lst, ["mI", "L0" + hs, "L1" + hs], ["wc" + hs, "xc" + hs], [b6])
+            if not last:
+                V("tt", ["xc" + hs, "DSC" + hs], ["XD" + hs], HS, 1.0, [b6], out=sl(T.XD, h), in0=ps(b6, 2), in1=sl(T.DSC, h), op=OP.mult)
+            MM([(ps(b6, 0), T.fI[:], sl(T.HK, h), True, False, HS, True), (ps(b6, 0), T.mNB[:], sl(T.DSC, h), False, False, HS, False)],
+               ["fI", "mNB", "HK" + hs, "DSC" + hs], ["key" + hs], [b6])
+            for c in range(4):
+                b = ring[0] % 4
+                ring[0] += 1
+                ks = range(4 * c, 4 * c + 4)
+                byS = c < CFG["es"]
+                lst = []
+                for j, k in enumerate(ks):
+                    lst.append((ps(b, j), T.mI[:], T.YG[:, h * 2048 + k:(h + 1) * 2048:16], True, not byS, HS, False))
+                    if byS:
+                        lst.append((ps(b, j), T.mNI[:], sl(L1, h), False, True, HS, False))
+                MM(lst, ygk + ["mI"] + (["mNI", "L1" + hs] if byS else []), ["ring%d" % b], [b])
+                if byS:
+                    A(["ring%d" % b], ["EA" + hs], 512, [b], out=T.EA[:, h * 512:(h + 1) * 512], in_=T["pb%d" % b][:, 0:512], func=AF.Abs)
+                    A(["EA" + hs], ["E%d_%d" % (h, k) for k in ks], 512, out=T.E[:, h * 2048 + c * 512:h * 2048 + (c + 1) * 512], in_=T.EA[:, h * 512:(h + 1) * 512],
+                      func=AF.Relu, scale=-1.0, bias=1.0)
+                for j, k in enumerate(ks if not byS else ()):
+                    V("tt", ["ring%d" % b, "L1" + hs], ["E%d_%d" % (h, k)], HS, 1.0, [b],
+                      out=T.E[:, h * 2048 + k * 128:h * 2048 + (k + 1) * 128], in0=ps(b, j), in1=sl(L1, h), op=OP.is_equal)
+                MM([(ps(b6, 0), T.SEL[:, k * 128:(k + 1) * 128], T.E[:, h * 2048 + k * 128:h * 2048 + (k + 1) * 128], False, k == 15, HS, False) for k in ks],
+                   ["SEL"] + ["E%d_%d" % (h, k) for k in ks], ["key" + hs], [b6])
+            V("tr", ["key" + hs], ["KT" + hs], HS, 1.0, [b6], out=sl(T.KT, h), in_=ps(b6, 0))
+            A(["key" + hs], ["KH" + hs], HS, [b6], out=sl(T.KH, h), in_=ps(b6, 0), func=AF.Relu, scale=-1.0)
+            V("scan", ["KT" + hs, "SD"], ["SC" + hs], HS, 1.0, out=sl(T.SC, h), data0=T.SD[:], data1=sl(T.KT, h), initial=-4096.0, op0=OP.add, op1=OP.max)
+            lst = []
+            for hh in range(2):
+                for g2 in range(2):
+                    lst.append((T["pb%d" % b6][:, 128 + hh:136:2], T.fP[:, (2 * hh + g2) * 128:(2 * hh + g2 + 1) * 128],
+                                T.SC[:, h * HS + g2 * 16 + 15:(h + 1) * HS:32], g2 == 0, g2 == 1, 4, True))
+            MM(lst, ["fP", "SC" + hs], ["mk" + hs], [b6])
+            ws = slice(8 * h, 8 * h + 8)
+            V("ts", ["mk" + hs], ["K32" + hs], 8, 1.0, [b6], out=T.K32[:, ws], in0=T["pb%d" % b6][:, 128:136], scalar1=131072.0, scalar2=None, op0=OP.mult)
+            V("ts", ["K32" + hs], ["N32" + hs], 8, out=T.N32[:, ws], in0=T.K32[:, ws], scalar1=4095, scalar2=None, op0=OP.bitwise_and)
+            V("cp", ["N32" + hs], ["NS" + hs], 8, out=NS[:, ws], in_=T.N32[:, ws])
+            send(t, "2%d" % h, spk, NS[:, ws], LN[:, ws], ["NS" + hs], ["LN" + hs], 1900)
+            V("tt", ["X", "NS" + hs, "L0" + hs], ["DM" + hs], HS, 1.5, (), 40, out=sl(T.DM, h), in0=T.X[:].indirect(NS[:, ws]), in1=m0(L0, h, 0), op=OP.not_equal)
+            if not last:
+                V("tt", ["X", "NS" + hs, "UND" + hs], ["YU" + hs], HS, 1.5, (), 40, out=sl(T.YU, h), in0=T.X[:].indirect(NS[:, ws]), in1=sl(T.UND, h), op=OP.mult)
+                V("ts", ["K32" + hs], ["KK" + hs], 8, out=T.KK[:, ws], in0=T.K32[:, ws], scalar1=12, scalar2=15, op0=OP.arith_shift_right, op1=OP.bitwise_and)
+                V("tt", ["KK" + hs, "CI"], ["OF" + hs], 8, out=T.OF[:, ws], in0=T.CI[:, ws], in1=T.KK[:, ws], op=OP.subtract)
+                V("cp", ["OF" + hs], ["OF16" + hs], 8, out=T.OF16[:, ws], in_=T.OF[:, ws])
+            V("tt", ["wc" + hs, "DM" + hs], ["DMW" + hs], HS, 1.0, [b6], out=sl(T.DMW, h), in0=ps(b6, 3), in1=sl(T.DM, h), op=OP.mult)
+            MM([(ps(b6, 2), T.mNB[:], sl(T.DM, h), True, False, HS, False), (ps(b6, 2), T.mI[:], m0(L0, h, 2), False, True, HS, False),
+                (ps(b6, 3), T.mTB[:], sl(T.DMW, h), True, True, HS, False)], ["mNB", "mI", "mTB", "DM" + hs, "DMW" + hs, "L0" + hs], ["tt" + hs, "wc" + hs, "xc" + hs], [b6])
+            A(["tt" + hs], ["TH" + hs], HS, [b6], out=sl(T.TH, h), in_=ps(b6, 2), func=AF.Relu, scale=2.0 ** 98)
+            V("tt", ["tt" + hs, "TH" + hs], ["FF%d_%d" % (t, h)], HS, 1.0, [b6], out=sl(FF, h), in0=ps(b6, 3), in1=sl(T.TH, h), op=OP.is_gt)
+            send(t, "3%d" % h, spk, sl(FF, h), sl(LF, h), ["FF%d_%d" % (t, h)], ["LF%d_%d" % (t, h)], 2000)
+        if not last:
+            for h in range(NH):
+                hs = str(h)
+                cur_h[0] = h
+                V("tt", ["YU" + hs, "XD" + hs, "OF16" + hs], ["X"], HS, 3.5, (), 40, out=T.X[:].indirect(T.OF16[:, 8 * h:8 * h + 8]),
+                  in0=sl(T.YU, h), in1=sl(T.XD, h), op=OP.add)
+        for h in range(NH):
+            hs = str(h)
+            cur_h[0] = h
+            b4, b6 = 4 + h, 6 + h
+            ws = slice(8 * h, 8 * h + 8)
+            V("tt", ["ASI", "LN" + hs, "KAP" + hs], ["CM" + hs], HS, 1.5, (), 40, out=sl(T.CM, h), in0=T.ASI[:].indirect(LN[:, ws]), in1=sl(T.KAP, h), op=OP.min)
+            V("tt", ["CM" + hs, "q" + hs], ["Cs" + hs], HS, 1.0, [b4], out=sl(T.C, h), in0=ps(b4, 2), in1=sl(T.CM, h), op=OP.max)
+            if not last:
+                V("cp", ["Cs" + hs], ["C16" + hs], HS, 1.0, out=sl(T.C16, h), in_=sl(T.C, h))
+            V("tt", ["ASH", "NS" + hs, "KH" + hs], ["HM" + hs], HS, 1.5, (), 40, out=sl(T.HM, h), in0=T.ASH[:].indirect(NS[:, ws]), in1=sl(T.KH, h), op=OP.min)
+            V("tt", ["HM" + hs, "key" + hs], ["HK" + hs], HS, 1.0, [b6], out=sl(T.HK, h), in0=ps(b6, 0), in1=sl(T.HM, h), op=OP.max)
+            if not last:
+                V("ts", ["HK" + hs, "cH"], ["H16" + hs], HS, 1.0, out=sl(T.H16, h), in0=sl(T.HK, h), scalar1=131072.0, scalar2=col(cH), op0=OP.mult, op1=OP.subtract)
+            else:
+                V("ts", ["HK" + hs, "cH"], ["OH" + hs], HS, 1.0, out=sl(T.OH, h), in0=sl(T.HK, h), scalar1=131072.0, scalar2=col(cH), op0=OP.mult, op1=OP.subtract)
+            MM([(ps(b4, 0), T.mI[:], sl(T.R, h), True, True, HS, False)], ["mI", "Rs" + hs], ["Sk" + hs], [b4])
+            cur, ck, pc, pk = T.R, "Rs" + hs, 0, "Sk" + hs
+            for role, (f, fk) in enumerate([(LF, "LF%d_%d" % (t, h)), (FF, "FF%d_%d" % (t, h))]):
+                V("tt", [pk, fk], ["MA" + hs], HS, 1.0, [b4], out=sl(T.MA, h), in0=ps(b4, pc), in1=sl(f, h), op=OP.mult)
+                MM([(ps(b4, 1), T.mB[:], sl(T.MA, h), True, True, HS, False)], ["mB", "MA" + hs], ["cnt" + hs, "dB" + hs], [b4])
+                V("tt", [ck, "cnt" + hs], ["LA" + hs], HS, 1.0, [b4], out=sl(T.LA, h), in0=ps(b4, 1), in1=sl(cur, h), op=OP.is_gt)
+                nc, nk = (2, "q" + hs) if role == 0 else (3, "t2" + hs)
+                MM([(ps(b4, nc), T.mI[:], sl(cur, h), True, False, HS, False), (ps(b4, nc), T.mNI[:], sl(T.MA, h), False, False, HS, False),
+                    (ps(b4, nc), T.mI[:], sl(T.LA, h), False, True, HS, False)], ["mI", "mNI", ck, "MA" + hs, "LA" + hs], [nk], [b4])
+                if role == 0:
+                    A([nk], ["Rq" + hs], HS, [b4], out=sl(T.R1, h), in_=ps(b4, nc), func=AF.Copy)
+                    cur, ck = T.R1, "Rq" + hs
+                elif not last:
+                    orders(h, t + 1, ps(b4, nc), [nk], [b4])
+                    A([nk], ["Rs" + hs], HS, [b4], out=sl(T.R, h), in_=ps(b4, nc), func=AF.Copy)
+                else:
+                    A([nk], ["OR" + hs], HS, [b4], out=sl(T.OR, h), in_=ps(b4, nc), func=AF.Copy)
+                pc, pk = nc, nk
+            lfs = ["LF%d_%d" % (u, h) for u in range(t + 1)]
+            if not last:
+                MM([(ps(b6, 1), T.mI[:], sl(T.Q0, h), True, False, HS, False)] + [(ps(b6, 1), T.mB[:], sl(T["LF_%d" % u], h), False, u == t, HS, False) for u in range(t + 1)],
+                   ["mI", "mB", "Q0"] + lfs, ["mk" + hs], [b6])
+                V("ts", ["mk" + hs], ["IND" + hs], HS, 1.0, [b6], out=sl(T.IND, h), in0=ps(b6, 1), scalar1=3.5, scalar2=-4.0, op0=OP.is_gt, op1=OP.mult)
+                MM([(ps(b6, 2), T.mI[:], sl(T.Q0, h), True, False, HS, False)] + [(ps(b6, 2), T.mB[:], sl(T["LF_%d" % u], h), False, False, HS, False) for u in range(t + 1)]
+                   + [(ps(b6, 2), T.mI[:], sl(T.IND, h), False, True, HS, False)], ["mI", "mB", "Q0", "IND" + hs] + lfs, ["tt" + hs, "xc" + hs], [b6])
+                A(["tt" + hs], ["th%d_%d" % (t + 1, h)], HS, [b6], out=m0(T["M0_%d" % (t + 1)], h, 2), in_=ps(b6, 2), func=AF.Copy, bias=6.5)
+            else:
+                MM([(ps(b6, 1), T.mI[:], sl(T.AB, h), True, False, HS, False)] + [(ps(b6, 1), T.mB[:], sl(T["LF_%d" % u], h), False, u == t, HS, False) for u in range(t + 1)],
+                   ["mI", "mB", "AB"] + lfs, ["mk" + hs], [b6])
+                A(["mk" + hs], ["OA" + hs], HS, [b6], out=sl(T.OA, h), in_=ps(b6, 1), func=AF.Copy)
+
+    def store(i, q, dst, src, rd):
+        e = g.sync if q == "Y" else g.scalar
+        add(q, lambda: e.dma_start(out=dst, in_=src), rd, ["out%d" % i], 60, sem="st_%d" % i, val=16, lat=2000)
+    for h in range(NH):
+        store(h, "Y", sl(T.yctx, h), sl(T.C, h), ["Cs%d" % h])
+        store(2 + h, "Y", sl(T.ycand, h), sl(T.OH, h), ["OH%d" % h])
+        store(4 + h, "Y", sl(T.ypref, h), sl(T.OR, h), ["OR%d" % h])
+        store(6 + h, "Y", sl(T.yfail, h), T.OA[0:128:16, h * HS:(h + 1) * HS], ["OA%d" % h])
+    return ops
+
+
+def depend(ops):
+    lastw, readers, lastb = {}, {}, {}
+    deps = []
+    for i, o in enumerate(ops):
+        d = {}
+        for k in o["rd"]:
+            for w in lastw.get(k, ()):
+                d[w] = True
+        for k in o["wr"]:
+            for w in lastw.get(k, ()):
+                d[w] = True
+            for r in readers.get(k, ()):
+                if r != i:
+                    d[r] = True
+        for b in o["bk"]:
+            if b in lastb:
+                d.setdefault(lastb[b], False)
+        if "after" in o:
+            d[o["after"]] = True
+        deps.append(d)
+        for k in o["rd"]:
+            readers.setdefault(k, []).append(i)
+        for k in o["wr"]:
+            lastw[k] = [i]
+            readers[k] = []
+        for b in o["bk"]:
+            lastb[b] = i
+    return deps
+
+
+BIAS = {}
+
+
+def klass(o):
+    w = o["wr"][0] if o["wr"] else "snd" + o["remote"][0].split("_")[1][0]
+    a = w.split("_")[0]
+    while a and a[-1].isdigit():
+        a = a[:-1]
+    return "%s%s%d" % (o["q"], a, o["h"])
+
+
+def schedule(ops, deps):
+    n = len(ops)
+    succ = [[] for _ in range(n)]
+    for i, d in enumerate(deps):
+        for j in d:
+            succ[j].append(i)
+    WAKE, alpha, win = CFG["wake"], CFG["alpha"], CFG["win"]
+    prio = [0.0] * n
+    for i in range(n - 1, -1, -1):
+        m = 0.0
+        for j in succ[i]:
+            m = max(m, prio[j] + (WAKE if ops[j]["q"] != ops[i]["q"] else 30.0))
+        prio[i] = m + ops[i]["cost"] + ops[i]["lat"]
+    for i in range(n):
+        if ops[i]["h"] == 0:
+            prio[i] += CFG["bonus"]
+        prio[i] += BIAS.get(klass(ops[i]), 0.0)
+    left = [len(d) for d in deps]
+    ready = [0.0] * n
+    fin = [0.0] * n
+    beg = [0.0] * n
+    avail = {}
+    free = {}
+    for i in range(n):
+        avail.setdefault(ops[i]["q"], [])
+        free.setdefault(ops[i]["q"], 0.0)
+        if left[i] == 0:
+            avail[ops[i]["q"]].append(i)
+    order = []
+    while True:
+        best = None
+        for q in avail:
+            if not avail[q]:
+                continue
+            fq = free[q] if q != "N" else 0.0
+            est = min(max(fq, ready[i]) for i in avail[q])
+            i, top = None, None
+            for z in avail[q]:
+                zs = max(fq, ready[z])
+                if zs <= est + win:
+                    sc = prio[z] - alpha * (zs - est)
+                    if top is None or sc > top:
+                        i, top = z, sc
+            st = max(fq, ready[i])
+            if best is None or st < best[0]:
+                best = (st, i, q)
+        if best is None:
+            break
+        st, i, q = best
+        avail[q].remove(i)
+        order.append(i)
+        beg[i] = st
+        free[q] = st + ops[i]["cost"]
+        fin[i] = st + ops[i]["cost"] + ops[i]["lat"]
+        for j in succ[i]:
+            ready[j] = max(ready[j], fin[i] + (WAKE if ops[j]["q"] != q else (30.0 if deps[j][i] else 0.0)))
+            left[j] -= 1
+            if left[j] == 0:
+                avail[ops[j]["q"]].append(j)
+    return order, beg, fin
+
+
+def rank_program(g, core, T, topo):
+    rank = T.rank_of(core)
+    if rank is None:
+        return
+    ops = build(g, T, topo, rank, core)
+    deps = depend(ops)
+    if "o" not in _ORDER:
+        _ORDER["o"] = schedule(ops, deps)[0]
+    order = _ORDER["o"]
+    eng = {"V": g.vector, "S": g.scalar, "T": g.tensor, "G": g, "Y": g.sync}
+    cnt = {}
+    done = {}
+    clock = {}
+    know = {q: {} for q in "VSTGY"}
+    for i in order:
+        o = ops[i]
+        q = o["q"]
+        if q == "N":
+            done[i] = (o["sem"], o["val"])
+            clock[i] = {o["sem"]: o["val"]}
+            cnt[o["sem"]] = o["val"]
+            continue
+        need = {}
+        for d, raw in deps[i].items():
+            od = ops[d]
+            if od["q"] == q and od["sem"] is None and (not raw or q in "TG"):
+                if not (q == "G"):
+                    continue
+                continue
+            s, v = done[d]
+            if know[q].get(s, 0) < v and (s not in need or need[s][0] < v):
+                need[s] = (v, d)
+        for s in list(need):
+            v, d = need[s]
+            for s2 in need:
+                if s2 != s and clock[need[s2][1]].get(s, 0) >= v:
+                    del need[s]
+                    break
+        for s in need:
+            v, d = need[s]
+            eng[q].wait_ge(T.sem[s], v)
+            for k, x in clock[d].items():
+                if know[q].get(k, 0) < x:
+                    know[q][k] = x
+        ins = o["fn"]()
+        if "remote" in o:
+            cnt[o["remote"][0]] = o["remote"][1]
+            done[i] = None
+            continue
+        s = o["sem"] or "s" + q
+        inc = o["val"] if o["sem"] else 1
+        ins.then_inc(T.sem[s], inc)
+        cnt[s] = cnt.get(s, 0) + inc
+        done[i] = (s, cnt[s])
+        c = dict(know[q])
+        c[s] = cnt[s]
+        if o["sem"] is None:
+            know_self = c
+        clock[i] = c
+    for s in cnt:
+        if know["G"].get(s, 0) < cnt[s]:
+            g.wait_ge(T.sem[s], cnt[s])

@@ -12,32 +12,34 @@ LN2 = math.log(2.0)
 WT = 85
 CFG = {"npc": 4,
        "vc": ((0, 3),),
+       "vc0": ((0, 3),),
        "vh": (),
-       "ns": 5,
-       "es": 1,
-       "bitV": True, "dbV": True, "alpha": 20.0, "win": 300.0,
-       "bonus": 1500.0, "g": 1.5, "f": 1.22, "ov": 12.0, "wake": 80.0, "hop": 2000.0}
+       "ns": (4, 4),
+       "es": (1, 1),
+       "nq": (1, 1),
+       "bitV": (1, 1), "alpha": 20.0, "win": 300.0,
+       "bonus": 1500.0, "g": 1.5, "f": 1.2, "ov": 12.0, "wake": 120.0, "hop": 2000.0}
 
 SCRATCH = {}
 for _n, _s, _d in [
     ("X", [128, W], "bfloat16"), ("ASI", [128, W], "int32"), ("ASH", [128, W], "float32"),
     ("XG", [128, W], "bfloat16"), ("YG", [128, W], "bfloat16"), ("DW", [128, W], "bfloat16"), ("E", [128, W], "bfloat16"), ("G", [128, W], "bfloat16"),
     ("CIN", [128, S], "int32"), ("HIN", [128, S], "int32"), ("RIN", [128, S], "int32"), ("FIN", [8, S], "int32"), ("Q8I", [8, S], "int32"),
-    ("A8", [8, S], "bfloat16"), ("Q8", [8, S], "bfloat16"), ("AB", [128, S], "bfloat16"), ("Q0", [128, S], "bfloat16"), ("IND", [128, S], "bfloat16"),
+    ("A8", [8, S], "bfloat16"), ("Q8", [8, S], "bfloat16"), ("AB", [128, S], "bfloat16"), ("IND", [128, S], "bfloat16"),
     ("C", [128, S], "float32"), ("C16", [128, S], "uint16"), ("HK", [128, S], "float32"), ("H16", [128, S], "uint16"),
     ("R", [128, S], "bfloat16"), ("R1", [128, S], "bfloat16"), ("MA", [128, S], "bfloat16"), ("LA", [128, S], "bfloat16"), ("IW", [128, S], "bfloat16"),
-    ("AB1", [128, S], "bfloat16"), ("BIT", [128, S], "bfloat16"), ("TI", [128, S], "int32"), ("SG", [128, S], "bfloat16"), ("KAP", [128, S], "bfloat16"),
+    ("AB1", [128, S], "bfloat16"), ("BIT", [128, S], "bfloat16"), ("TI", [128, S], "int32"), ("TJ", [128, S], "int32"), ("KAP", [128, S], "bfloat16"),
     ("CM", [128, S], "float32"), ("KH", [128, S], "float32"), ("HM", [128, S], "float32"), ("UND", [128, S], "bfloat16"), ("DSC", [128, S], "bfloat16"),
     ("XD", [128, S], "bfloat16"), ("YU", [128, S], "bfloat16"), ("KT", [128, S], "float32"), ("SC", [128, S], "float32"),
     ("K32", [128, 16], "int32"), ("N32", [128, 16], "int32"), ("KK", [128, 16], "int32"), ("OF", [128, 16], "int32"), ("OF16", [128, 16], "uint16"),
     ("DM", [128, S], "bfloat16"), ("DMW", [128, S], "bfloat16"), ("TH", [128, S], "float32"),
     ("OC", [128, S], "float32"), ("OH", [128, S], "float32"), ("OR", [128, S], "float32"), ("OA", [128, S], "float32"),
-    ("IP", [128, 1], "int32"), ("KI", [128, 1], "int32"), ("B4I", [128, 1], "int32"), ("COL", [128, 16], "float32"), ("COL2", [128, 2], "float32"), ("EA", [128, 1024], "bfloat16"), ("COLB", [128, 2], "bfloat16"),
-    ("IM", [128, 128], "float32"), ("IMG", [128, 128], "float32"), ("IMK", [128, 128], "float32"), ("JS", [128, 2048], "bfloat16"),
+    ("IP", [128, 1], "int32"), ("KI", [128, 1], "int32"), ("B4I", [128, 1], "int32"), ("COL", [128, 16], "float32"), ("COL2", [128, 2], "float32"), ("EA", [128, 1024], "bfloat16"), ("CNH", [128, 1024], "bfloat16"), ("THC", [128, 16], "float32"), ("COLB", [128, 2], "bfloat16"),
+    ("IM", [128, 128], "float32"), ("IMG", [128, 128], "float32"), ("IMK", [128, 128], "float32"), ("IMB", [128, 128], "bfloat16"),
     ("SEL", [128, 2048], "bfloat16"), ("CNT", [128, 2048], "bfloat16"),
     ("mB", [128, 128], "bfloat16"), ("mI", [128, 128], "bfloat16"), ("mNI", [128, 128], "bfloat16"), ("mNB", [128, 128], "bfloat16"),
     ("mTB", [128, 128], "bfloat16"), ("mWB", [128, 128], "bfloat16"), ("mCW", [128, 128], "bfloat16"), ("mKC", [128, 128], "bfloat16"),
-    ("mHF", [128, 128], "bfloat16"), ("ONES", [128, 128], "bfloat16"), ("mI2", [128, 128], "bfloat16"), ("TMP", [128, 128], "float32"), ("MK0", [128, 128], "float32"),
+    ("mNW", [128, 128], "bfloat16"), ("m4", [128, 128], "bfloat16"), ("ONES", [128, 128], "bfloat16"), ("mI2", [128, 128], "bfloat16"), ("TMP", [128, 128], "float32"), ("MK0", [128, 128], "float32"),
     ("fI", [128, 128], "float32"), ("fP", [128, 512], "float32"), ("SD", [128, 128], "float32"), ("CII", [128, 16], "int32"), ("CI", [128, 16], "int32"),
     ("mG8", [8, 128], "bfloat16"),
 ]:
@@ -121,7 +123,8 @@ def build(g, T, topo, rank, core):
     ldw("Y", "pref", "RIN", T.RIN[:], T.pref[:], 2300)
     ldw("Y", "cand", "HIN", T.HIN[:], T.cand[:], 2400)
     ldw("Y", "fail0", "FIN", T.FIN[:], T.fail0[:], 2400)
-    ldw("S", "assoc", "ASI", T.ASI[:], T.assoc[:], 8500)
+    ldw("S", "assoc", "ASI", T.ASI[:], T.assoc[:], 6500)
+    ops[-1]["rd"] = ["X"]
 
     def iota(dst, key, pattern, base, cm, n, flag=True):
         if flag:
@@ -133,7 +136,7 @@ def build(g, T, topo, rank, core):
     iota(T.IP[:], "IP", [[1, 1]], 0, 1, 1, False)
     iota(T.IM[:], "IM", [[1, 128]], 0, 0, 128)
     iota(T.IMG[:], "IMG", [[16, 8], [0, 16]], 0, 0, 128)
-    iota(T.JS[:], "JS", [[-1, 16], [1, 128]], 0, 0, 2048)
+    iota(T.IMB[:], "IMB", [[1, 128]], 0, 0, 128)
     iota(T.IMK[:], "IMK", [[0, 8], [1, 16]], 0, 0, 128)
     iota(T.CII[:], "CII", [[256, 16]], 15, 0, 16, False)
 
@@ -161,34 +164,42 @@ def build(g, T, topo, rank, core):
     def orders(h, t, src, rd, banks=()):
         A(rd, ["w%d_%d" % (t, h)], HS, banks, out=m0(T["M0_%d" % t], h, 1), in_=src, func=AF.Exp, bias=col(12), scale=-11.0 * LN2)
         ops[-1]["rd"].append("bias")
-        A(rd + ["bias"], ["IW%d" % h], HS, banks, out=sl(T.IW, h), in_=src, func=AF.Exp, bias=col(13), scale=LN2)
+        A(rd, ["IW%d" % h], HS, banks, out=sl(T.IW, h), in_=src, func=AF.Exp, scale=LN2)
 
     add("V", lambda: g.vector.memset(col(12), WT * LN2), [], ["bias"], 80)
-    add("V", lambda: g.vector.memset(col(13), -16.0 * LN2), [], ["bias"], 80)
+    add("V", lambda: g.vector.memset(col(13), 6.5 * 2.0 ** 96), [], ["bias"], 80)
     add("V", lambda: g.vector.memset(col(14), 15.0 * LN2), [], ["bias"], 80)
     for h in range(NH):
         orders(h, 0, sl(T.R, h), ["Rs%d" % h])
 
-    mat(T.SEL[:], "SEL", T.JS[:], "JS", col(cG16), "cG16", 2048, 0.5)
+    for k in range(16):
+        V("ts", ["IMB", "cG16"], ["SEL%d" % (k // 4)], 128, 0.5, out=T.SEL[:, k * 128:(k + 1) * 128], in0=T.IMB[:], scalar1=float(k), scalar2=col(cG16), op0=OP.subtract, op1=OP.is_equal)
     for j in range(4):
-        MM([(T["pb%d" % j][:, 0:512], T.mI[:], T.SEL[:, j * 512:(j + 1) * 512], True, True, 512, False)], ["mI", "SEL"], ["ring%d" % j], [j])
+        MM([(T["pb%d" % j][:, 0:512], T.mI[:], T.SEL[:, j * 512:(j + 1) * 512], True, True, 512, False)], ["mI", "SEL%d" % j], ["ring%d" % j], [j])
         m = 512 if j < 3 else 384
-        V("tt", ["SEL", "ring%d" % j], ["CNT"], m, 1.0, [j], out=T.CNT[:, j * 512:j * 512 + m], in0=T["pb%d" % j][:, 0:m], in1=T.SEL[:, j * 512 + 128:j * 512 + 128 + m], op=OP.subtract)
-    V("cp", ["SEL"], ["CNT"], 128, 0.5, out=T.CNT[:, 1920:2048], in_=T.SEL[:, 1920:2048])
+        V("tt", ["SEL%d" % j, "SEL%d" % min(j + 1, 3), "ring%d" % j], ["CNT%d" % j], m, 1.0, [j], out=T.CNT[:, j * 512:j * 512 + m], in0=T["pb%d" % j][:, 0:m], in1=T.SEL[:, j * 512 + 128:j * 512 + 128 + m], op=OP.subtract)
+    V("cp", ["SEL3"], ["CNT3"], 128, 0.5, out=T.CNT[:, 1920:2048], in_=T.SEL[:, 1920:2048])
     ns = CFG["ns"]
-    if ns:
-        V("ts", ["CNT"], ["CNT"], 128 * ns, 0.5, out=T.CNT[:, 0:128 * ns], in0=T.CNT[:, 0:128 * ns], scalar1=0.5, scalar2=None, op0=OP.mult)
-        V("ts", ["cK"], ["c8a"], 1, out=T.COL2[:, 0:1], in0=col(cK), scalar1=0.0, scalar2=8.0, op0=OP.is_equal, op1=OP.mult)
-        V("ts", ["cK"], ["c8b"], 1, out=T.COL2[:, 1:2], in0=col(cK), scalar1=float(ns), scalar2=8.0, op0=OP.is_equal, op1=OP.mult)
-        V("tt", ["c8a", "c8b"], ["c8"], 1, out=col(15), in0=T.COL2[:, 0:1], in1=T.COL2[:, 1:2], op=OP.subtract)
-    else:
-        add("V", lambda: g.vector.memset(col(15), 0.0), [], ["c8"], 80)
+    nx = max(ns)
+    allcnt = ["CNT%d" % j for j in range(4)]
+    allsel = ["SEL%d" % j for j in range(4)]
+    V("ts", allcnt, ["CNH"], 128 * nx, 0.5, out=T.CNH[:, 0:128 * nx], in0=T.CNT[:, 128 * (16 - nx):], scalar1=0.5, scalar2=None, op0=OP.mult)
+    for h in range(NH):
+        V("ts", ["cK"], ["c8%d" % h], 1, out=T.COL2[:, h:h + 1], in0=col(cK), scalar1=float(16 - ns[h]), scalar2=8.0, op0=OP.is_equal, op1=OP.mult)
+    for r in range(16 - nx, 16):
+        add("V", lambda r=r: g.vector.memset(T.THC[:, r:r + 1], -0.6 * 2.0 ** (WT - 11 * r)), [], ["thr%d" % r], 65)
+
+    def cntm(r, h):
+        if r >= 16 - ns[h]:
+            return T.CNH[:, 128 * (r - 16 + nx):128 * (r - 15 + nx)]
+        return T.CNT[:, 128 * r:128 * (r + 1)]
     mat(T.mB[:], "mB", T.IMG[:], "IMG", col(cG16), "cG16")
     add("V", lambda: g.vector.memset(T.ONES[:], 1.0), [], ["ONES"], 80)
     A(["cK", "bias"], ["cb2"], 1, out=T.COLB[:, 0:1], in_=col(cK), func=AF.Exp, bias=col(14), scale=-LN2)
     A(["cK", "bias"], ["cbw"], 1, out=T.COLB[:, 1:2], in_=col(cK), func=AF.Exp, bias=col(12), scale=-11.0 * LN2)
     V("ts", ["mB", "cb2"], ["mWB"], 128, 1.0, out=T.mWB[:], in0=T.mB[:], scalar1=T.COLB[:, 0:1], scalar2=None, op0=OP.mult)
-    V("ts", ["mI"], ["mHF"], 128, 0.5, out=T.mHF[:], in0=T.mI[:], scalar1=0.5, scalar2=None, op0=OP.mult)
+    V("ts", ["mWB"], ["mNW"], 128, 0.5, out=T.mNW[:], in0=T.mWB[:], scalar1=-1.0, scalar2=None, op0=OP.mult)
+    V("ts", ["mI"], ["m4"], 128, 0.5, out=T.m4[:], in0=T.mI[:], scalar1=-4.0, scalar2=None, op0=OP.mult)
     V("cp", ["HIN"], ["H160", "H161"], S, out=T.H16[:], in_=T.HIN[:])
     V("ts", ["mB", "cbw"], ["TMP"], 128, 1.0, out=T.TMP[:], in0=T.mB[:], scalar1=T.COLB[:, 1:2], scalar2=-0.6, op0=OP.mult, op1=OP.mult)
     V("ts", ["IMK"], ["MK0"], 128, 1.0, out=T.MK0[:], in0=T.IMK[:], scalar1=0.5, scalar2=None, op0=OP.is_gt)
@@ -220,9 +231,9 @@ def build(g, T, topo, rank, core):
     MM([(T.pb6[:, 0:256], T.mG8[:], T.A8[:], True, True, S, False), (T.pb6[:, 256:512], T.mG8[:], T.Q8[:], True, True, S, False)],
        ["mG8", "A8", "Q8"], ["b6a"], [6])
     A(["b6a"], ["AB"], S, [6], out=T.AB[:], in_=T.pb6[:, 0:256], func=AF.Copy)
-    A(["b6a"], ["Q0"], S, [6], out=T.Q0[:], in_=T.pb6[:, 256:512], func=AF.Copy)
     for h in range(NH):
-        A(["Q0"], ["th0_%d" % h], HS, out=m0(T.M0_0, h, 2), in_=sl(T.Q0, h), func=AF.Copy, bias=6.5)
+        A(["b6a"], ["th0_%d" % h], HS, [6], out=m0(T.M0_0, h, 2), in_=T.pb6[:, 256 + h * HS:256 + (h + 1) * HS], func=AF.Copy)
+
     for j in range(8):
         V("ts", ["ASI", "cH"], ["ASH"], W // 8, 1.0, out=T.ASH[:, j * 512:(j + 1) * 512], in0=T.ASI[:, j * 512:(j + 1) * 512],
           scalar1=col(cH), scalar2=2.0 ** -17, op0=OP.add, op1=OP.mult)
@@ -266,59 +277,67 @@ def build(g, T, topo, rank, core):
         for h in range(NH):
             hs = str(h)
             cur_h[0] = h
-            gather(t, h, T.C16, T.XG, "XG", "C16", CFG["vc"])
+            gather(t, h, T.C16, T.XG, "XG", "C16", CFG["vc"] if t else CFG["vc0"])
             xgk = ["XG%d%d" % (h, j) for j in range(CFG["npc"])]
 
-            def xg(k, h=h):
-                return T.XG[:, h * 2048 + k:(h + 1) * 2048:16]
             b4 = 4 + h
-            V("cp", xgk, ["x0_%d" % h], HS, 0.5, out=m0(M0, h, 0), in_=xg(0))
-            for c in range(4):
-                ks = range(1 + 4 * c, min(16, 5 + 4 * c))
-                b = ring[0] % 4
-                ring[0] += 1
-                lst = []
-                for j, k in enumerate(ks):
-                    lst.append((ps(b, j), T.mI[:], xg(k), True, False, HS, False))
-                    lst.append((ps(b, j), T.mNI[:], xg(0), False, True, HS, False))
-                MM(lst, xgk + ["mI", "mNI"], ["ring%d" % b], [b])
-                for j, k in enumerate(ks):
-                    V("tt", ["ring%d" % b, "w%d_%d" % (t, h)], ["DW%d_%d" % (h, k)], HS, 1.0, [b],
-                      out=T.DW[:, h * 2048 + k * 128:h * 2048 + (k + 1) * 128], in0=ps(b, j), in1=m0(M0, h, 1), op=OP.mult)
-                MM([(ps(b4, 0), T.SEL[:, k * 128:(k + 1) * 128], T.DW[:, h * 2048 + k * 128:h * 2048 + (k + 1) * 128], k == 1, k == 15, HS, False) for k in ks],
-                   ["SEL"] + ["DW%d_%d" % (h, k) for k in ks], ["Sk" + hs], [b4])
+            nq = CFG["nq"][h]
+            qs = HS // nq
+            npq = CFG["npc"] // nq
+            V("cp", xgk, ["x0_%d" % h], HS, 0.5, out=m0(M0, h, 0), in_=T.XG[:, h * 2048:(h + 1) * 2048:16])
+            for q in range(nq):
+                qk = xgk[q * npq:(q + 1) * npq]
+
+                def xg(k, h=h, q=q, qs=qs):
+                    return T.XG[:, h * 2048 + q * qs * 16 + k:h * 2048 + (q + 1) * qs * 16:16]
+
+                def dw(k, h=h, q=q, qs=qs):
+                    return T.DW[:, h * 2048 + k * 128 + q * qs:h * 2048 + k * 128 + (q + 1) * qs]
+                wq = M0[:, (3 * h + 1) * HS + q * qs:(3 * h + 1) * HS + (q + 1) * qs]
+                sk = T["pb%d" % b4][:, q * qs:(q + 1) * qs]
+                nk = 512 // qs
+                for c in range(16 // nk):
+                    ks = range(1 + nk * c, min(16, 1 + nk + nk * c))
+                    b = ring[0] % 4
+                    ring[0] += 1
+                    for s0 in range(0, len(ks), 4):
+                        lst = []
+                        for j in range(s0, min(s0 + 4, len(ks))):
+                            o = T["pb%d" % b][:, j * qs:(j + 1) * qs]
+                            lst.append((o, T.mI[:], xg(ks[j]), True, False, qs, False))
+                            lst.append((o, T.mNI[:], xg(0), False, True, qs, False))
+                        MM(lst, qk + ["mI", "mNI"], ["ring%d" % b], [b])
+                    for j, k in enumerate(ks):
+                        V("tt", ["ring%d" % b, "w%d_%d" % (t, h)], ["DW%d%d_%d" % (h, q, k)], qs, 1.0, [b],
+                          out=dw(k), in0=T["pb%d" % b][:, j * qs:(j + 1) * qs], in1=wq, op=OP.mult)
+                    MM([(sk, T.SEL[:, k * 128:(k + 1) * 128], dw(k), k == 1, k == 15, qs, False) for k in ks],
+                       allsel + ["DW%d%d_%d" % (h, q, k) for k in ks], ["Sk" + hs], [b4])
             A(["Sk" + hs], ["ABS" + hs], HS, [b4], out=sl(T.AB1, h), in_=ps(b4, 0), func=AF.Abs)
 
             def G(r, h=h):
                 return T.G[:, h * 2048 + r * 128:h * 2048 + (r + 1) * 128]
             for r in range(16):
-                if r < CFG["ns"]:
-                    A(["ABS" + hs], ["G%d_%d" % (h, r)], HS, out=G(r), in_=sl(T.AB1, h), func=AF.Sign, scale=2.0 ** (11 * r - WT) / 0.6, bias=-1.0)
+                if r >= 16 - CFG["ns"][h]:
+                    A(["ABS" + hs, "thr%d" % r], ["G%d_%d" % (h, r)], HS, out=G(r), in_=sl(T.AB1, h), func=AF.Sign, bias=T.THC[:, r:r + 1])
                 else:
                     V("ts", ["ABS" + hs], ["G%d_%d" % (h, r)], HS, 0.5, out=G(r), in0=sl(T.AB1, h), scalar1=0.6 * 2.0 ** (WT - 11 * r), scalar2=None, op0=OP.is_ge)
                 if r % 4 == 3:
-                    MM([(ps(b4, 1), T.CNT[:, q * 128:(q + 1) * 128], G(q), q == 0, q == 15, HS, False) for q in range(r - 3, r + 1)],
-                       ["CNT"] + ["G%d_%d" % (h, q) for q in range(r - 3, r + 1)], ["cnt" + hs], [b4])
-            if CFG["bitV"]:
-                V("ts", ["cnt" + hs, "c8"], ["BIT" + hs], HS, 1.0, [b4], out=sl(T.BIT, h), in0=ps(b4, 1), scalar1=col(15), scalar2=0.5, op0=OP.add, op1=OP.is_gt)
+                    MM([(ps(b4, 1), cntm(q, h), G(q), q == 0, q == 15, HS, False) for q in range(r - 3, r + 1)],
+                       allcnt + ["CNH"] + ["G%d_%d" % (h, q) for q in range(r - 3, r + 1)], ["cnt" + hs], [b4])
+            c8 = T.COL2[:, h:h + 1]
+            if CFG["bitV"][h]:
+                V("ts", ["cnt" + hs, "c8" + hs], ["BIT" + hs], HS, 1.0, [b4], out=sl(T.BIT, h), in0=ps(b4, 1), scalar1=c8, scalar2=0.5, op0=OP.add, op1=OP.is_gt)
             else:
-                A(["cnt" + hs, "c8"], ["BIT" + hs], HS, [b4], out=sl(T.BIT, h), in_=ps(b4, 1), func=AF.Sign, bias=col(15))
-            MM([(ps(b4, 0), T.mHF[:], T.ONES[:], True, False, HS, False), (ps(b4, 0), T.mWB[:], sl(T.BIT, h), False, True, HS, False)],
-               ["mHF", "mWB", "ONES", "BIT" + hs], ["Sk" + hs], [b4])
-            V("tt", ["Sk" + hs, "IW" + hs], ["t2" + hs], HS, 1.0, [b4], out=ps(b4, 3), in0=ps(b4, 0), in1=sl(T.IW, h), op=OP.mult)
-            V("cp", ["t2" + hs], ["TI" + hs], HS, 1.0, [b4], out=sl(T.TI, h), in_=ps(b4, 3))
-            V("tt", ["t2" + hs, "TI" + hs], ["q" + hs], HS, 1.0, [b4], out=ps(b4, 2), in0=ps(b4, 3), in1=sl(T.TI, h), op=OP.subtract)
-            if CFG["dbV"]:
-                V("ts", ["q" + hs], ["dB" + hs], HS, 1.0, [b4], out=ps(b4, 1), in0=ps(b4, 2), scalar1=2.0 ** 28, scalar2=None, op0=OP.mult)
-            else:
-                A(["q" + hs], ["dB" + hs], HS, [b4], out=ps(b4, 1), in_=ps(b4, 2), func=AF.Copy, scale=2.0 ** 28)
-            ops[-1]["wr"].append("cnt" + hs)
-            V("tt", ["dB" + hs, "x0_%d" % h], ["x0p%d" % h], HS, 1.0, [b4], out=sl(M1, h), in0=ps(b4, 1), in1=m0(M0, h, 0), op=OP.max)
-            send(t, "1%d" % h, hear, sl(M1, h), sl(L1, h), ["x0p%d" % h], ["L1" + hs], 2000)
+                A(["cnt" + hs, "c8" + hs], ["BIT" + hs], HS, [b4], out=sl(T.BIT, h), in_=ps(b4, 1), func=AF.Sign, bias=c8)
+            MM([(ps(b4, 0), T.mWB[:], T.ONES[:], True, False, HS, False), (ps(b4, 0), T.mNW[:], sl(T.BIT, h), False, True, HS, False)],
+               ["mNW", "mWB", "ONES", "BIT" + hs], ["Sk" + hs], [b4])
+            V("tt", ["Sk" + hs, "IW" + hs], ["TI" + hs], HS, 1.0, [b4], out=sl(T.TI, h), in0=ps(b4, 0), in1=sl(T.IW, h), op=OP.mult)
+            V("ts", ["TI" + hs], ["TJ" + hs], HS, 1.0, out=sl(T.TJ, h), in0=sl(T.TI, h), scalar1=32768, scalar2=None, op0=OP.bitwise_and)
+            V("tt", ["TJ" + hs, "x0_%d" % h], ["x0p%d" % h], HS, 2.0, out=sl(M1, h), in0=m0(M0, h, 0), in1=sl(T.TJ, h), op=OP.add)
+            send(t, "1%d" % h, hear, sl(M1, h), sl(L1, h), ["x0p%d" % h], ["L1" + hs], CFG["hop"])
             MM([(ps(b4, 1), T.mI[:], sl(T.AB1, h), True, False, HS, False), (ps(b4, 1), T.mCW[:], sl(T.BIT, h), False, False, HS, False),
                 (ps(b4, 1), T.mKC[:], T.ONES[:], False, True, HS, False)], ["ABS" + hs, "mI", "mCW", "mKC", "ONES", "BIT" + hs], ["cnt" + hs, "dB" + hs], [b4])
-            A(["cnt" + hs], ["SG" + hs], HS, [b4], out=sl(T.SG, h), in_=ps(b4, 1), func=AF.Sign)
-            A(["SG" + hs], ["KAP" + hs], HS, out=sl(T.KAP, h), in_=sl(T.SG, h), func=AF.Relu, scale=8192.0)
+            V("ts", ["cnt" + hs], ["KAP" + hs], HS, 1.0, [b4], out=sl(T.KAP, h), in0=ps(b4, 1), scalar1=0.0, scalar2=8192.0, op0=OP.is_gt, op1=OP.mult)
             MM([(ps(b4, 2), T.fI[:], sl(T.C, h), True, False, HS, True), (ps(b4, 2), T.mNI[:], sl(T.KAP, h), False, True, HS, False)],
                ["fI", "mNI", "Cs" + hs, "KAP" + hs], ["q" + hs], [b4])
             send(t, "0%d" % h, hear, M0[:, h * 3 * HS:(h + 1) * 3 * HS], L0[:, h * 3 * HS:(h + 1) * 3 * HS], ["x0_" + hs, "w%d_%d" % (t, h), "th%d_%d" % (t, h)], ["L0" + hs], CFG["hop"] + 200)
@@ -344,7 +363,7 @@ def build(g, T, topo, rank, core):
                 b = ring[0] % 4
                 ring[0] += 1
                 ks = range(4 * c, 4 * c + 4)
-                byS = c < CFG["es"]
+                byS = c >= 4 - CFG["es"][h]
                 lst = []
                 for j, k in enumerate(ks):
                     lst.append((ps(b, j), T.mI[:], T.YG[:, h * 2048 + k:(h + 1) * 2048:16], True, not byS, HS, False))
@@ -359,7 +378,7 @@ def build(g, T, topo, rank, core):
                     V("tt", ["ring%d" % b, "L1" + hs], ["E%d_%d" % (h, k)], HS, 1.0, [b],
                       out=T.E[:, h * 2048 + k * 128:h * 2048 + (k + 1) * 128], in0=ps(b, j), in1=sl(L1, h), op=OP.is_equal)
                 MM([(ps(b6, 0), T.SEL[:, k * 128:(k + 1) * 128], T.E[:, h * 2048 + k * 128:h * 2048 + (k + 1) * 128], False, k == 15, HS, False) for k in ks],
-                   ["SEL"] + ["E%d_%d" % (h, k) for k in ks], ["key" + hs], [b6])
+                   allsel + ["E%d_%d" % (h, k) for k in ks], ["key" + hs], [b6])
             V("tr", ["key" + hs], ["KT" + hs], HS, 1.0, [b6], out=sl(T.KT, h), in_=ps(b6, 0))
             A(["key" + hs], ["KH" + hs], HS, [b6], out=sl(T.KH, h), in_=ps(b6, 0), func=AF.Relu, scale=-1.0)
             V("scan", ["KT" + hs, "SD"], ["SC" + hs], HS, 1.0, out=sl(T.SC, h), data0=T.SD[:], data1=sl(T.KT, h), initial=-4096.0, op0=OP.add, op1=OP.max)
@@ -373,24 +392,25 @@ def build(g, T, topo, rank, core):
             V("ts", ["mk" + hs], ["K32" + hs], 8, 1.0, [b6], out=T.K32[:, ws], in0=T["pb%d" % b6][:, 128:136], scalar1=131072.0, scalar2=None, op0=OP.mult)
             V("ts", ["K32" + hs], ["N32" + hs], 8, out=T.N32[:, ws], in0=T.K32[:, ws], scalar1=4095, scalar2=None, op0=OP.bitwise_and)
             V("cp", ["N32" + hs], ["NS" + hs], 8, out=NS[:, ws], in_=T.N32[:, ws])
-            send(t, "2%d" % h, spk, NS[:, ws], LN[:, ws], ["NS" + hs], ["LN" + hs], 1900)
-            V("tt", ["X", "NS" + hs, "L0" + hs], ["DM" + hs], HS, 1.5, (), 40, out=sl(T.DM, h), in0=T.X[:].indirect(NS[:, ws]), in1=m0(L0, h, 0), op=OP.not_equal)
+            send(t, "2%d" % h, spk, NS[:, ws], LN[:, ws], ["NS" + hs], ["LN" + hs], CFG["hop"] - 100)
+            V("ts", ["K32" + hs], ["KK" + hs], 8, out=T.KK[:, ws], in0=T.K32[:, ws], scalar1=12, scalar2=15, op0=OP.arith_shift_right, op1=OP.bitwise_and)
+            V("tt", ["KK" + hs, "CI"], ["OF" + hs], 8, out=T.OF[:, ws], in0=T.CI[:, 0:8], in1=T.KK[:, ws], op=OP.subtract)
+            V("cp", ["OF" + hs], ["OF16" + hs], 8, out=T.OF16[:, ws], in_=T.OF[:, ws])
+            ysrc = T.YG[:, h * 2048:(h + 1) * 2048].indirect(T.OF16[:, ws])
             if not last:
-                V("tt", ["X", "NS" + hs, "UND" + hs], ["YU" + hs], HS, 1.5, (), 40, out=sl(T.YU, h), in0=T.X[:].indirect(NS[:, ws]), in1=sl(T.UND, h), op=OP.mult)
-                V("ts", ["K32" + hs], ["KK" + hs], 8, out=T.KK[:, ws], in0=T.K32[:, ws], scalar1=12, scalar2=15, op0=OP.arith_shift_right, op1=OP.bitwise_and)
-                V("tt", ["KK" + hs, "CI"], ["OF" + hs], 8, out=T.OF[:, ws], in0=T.CI[:, ws], in1=T.KK[:, ws], op=OP.subtract)
-                V("cp", ["OF" + hs], ["OF16" + hs], 8, out=T.OF16[:, ws], in_=T.OF[:, ws])
+                V("tt", ygk + ["OF16" + hs, "UND" + hs], ["YU" + hs], HS, GR, (), 40, out=sl(T.YU, h), in0=ysrc, in1=sl(T.UND, h), op=OP.mult)
+            V("tt", ygk + ["OF16" + hs, "L0" + hs], ["DM" + hs], HS, GR, (), 40, out=sl(T.DM, h), in0=ysrc, in1=m0(L0, h, 0), op=OP.not_equal)
             V("tt", ["wc" + hs, "DM" + hs], ["DMW" + hs], HS, 1.0, [b6], out=sl(T.DMW, h), in0=ps(b6, 3), in1=sl(T.DM, h), op=OP.mult)
             MM([(ps(b6, 2), T.mNB[:], sl(T.DM, h), True, False, HS, False), (ps(b6, 2), T.mI[:], m0(L0, h, 2), False, True, HS, False),
                 (ps(b6, 3), T.mTB[:], sl(T.DMW, h), True, True, HS, False)], ["mNB", "mI", "mTB", "DM" + hs, "DMW" + hs, "L0" + hs], ["tt" + hs, "wc" + hs, "xc" + hs], [b6])
-            A(["tt" + hs], ["TH" + hs], HS, [b6], out=sl(T.TH, h), in_=ps(b6, 2), func=AF.Relu, scale=2.0 ** 98)
+            A(["tt" + hs, "bias"], ["TH" + hs], HS, [b6], out=sl(T.TH, h), in_=ps(b6, 2), func=AF.Relu, scale=2.0 ** 96, bias=col(13))
             V("tt", ["tt" + hs, "TH" + hs], ["FF%d_%d" % (t, h)], HS, 1.0, [b6], out=sl(FF, h), in0=ps(b6, 3), in1=sl(T.TH, h), op=OP.is_gt)
-            send(t, "3%d" % h, spk, sl(FF, h), sl(LF, h), ["FF%d_%d" % (t, h)], ["LF%d_%d" % (t, h)], 2000)
+            send(t, "3%d" % h, spk, sl(FF, h), sl(LF, h), ["FF%d_%d" % (t, h)], ["LF%d_%d" % (t, h)], CFG["hop"])
         if not last:
             for h in range(NH):
                 hs = str(h)
                 cur_h[0] = h
-                V("tt", ["YU" + hs, "XD" + hs, "OF16" + hs], ["X"], HS, 3.5, (), 40, out=T.X[:].indirect(T.OF16[:, 8 * h:8 * h + 8]),
+                V("tt", ["YU" + hs, "XD" + hs, "OF16" + hs], ["X"], HS, 3.5, (), 40, out=T.X[:, h * 2048:(h + 1) * 2048].indirect(T.OF16[:, 8 * h:8 * h + 8]),
                   in0=sl(T.YU, h), in1=sl(T.XD, h), op=OP.add)
         for h in range(NH):
             hs = str(h)
@@ -407,8 +427,9 @@ def build(g, T, topo, rank, core):
                 V("ts", ["HK" + hs, "cH"], ["H16" + hs], HS, 1.0, out=sl(T.H16, h), in0=sl(T.HK, h), scalar1=131072.0, scalar2=col(cH), op0=OP.mult, op1=OP.subtract)
             else:
                 V("ts", ["HK" + hs, "cH"], ["OH" + hs], HS, 1.0, out=sl(T.OH, h), in0=sl(T.HK, h), scalar1=131072.0, scalar2=col(cH), op0=OP.mult, op1=OP.subtract)
-            MM([(ps(b4, 0), T.mI[:], sl(T.R, h), True, True, HS, False)], ["mI", "Rs" + hs], ["Sk" + hs], [b4])
-            cur, ck, pc, pk = T.R, "Rs" + hs, 0, "Sk" + hs
+            if t == 0:
+                MM([(ps(b4, 3), T.mI[:], sl(T.R, h), True, True, HS, False)], ["mI", "Rs" + hs], ["t2" + hs], [b4])
+            cur, ck, pc, pk = T.R, "Rs" + hs, 3, "t2" + hs
             for role, (f, fk) in enumerate([(LF, "LF%d_%d" % (t, h)), (FF, "FF%d_%d" % (t, h))]):
                 V("tt", [pk, fk], ["MA" + hs], HS, 1.0, [b4], out=sl(T.MA, h), in0=ps(b4, pc), in1=sl(f, h), op=OP.mult)
                 MM([(ps(b4, 1), T.mB[:], sl(T.MA, h), True, True, HS, False)], ["mB", "MA" + hs], ["cnt" + hs, "dB" + hs], [b4])
@@ -427,12 +448,12 @@ def build(g, T, topo, rank, core):
                 pc, pk = nc, nk
             lfs = ["LF%d_%d" % (u, h) for u in range(t + 1)]
             if not last:
-                MM([(ps(b6, 1), T.mI[:], sl(T.Q0, h), True, False, HS, False)] + [(ps(b6, 1), T.mB[:], sl(T["LF_%d" % u], h), False, u == t, HS, False) for u in range(t + 1)],
-                   ["mI", "mB", "Q0"] + lfs, ["mk" + hs], [b6])
+                q0, qk = m0(M0, h, 2), "th%d_%d" % (t, h)
+                MM([(ps(b6, 1), T.mI[:], q0, True, False, HS, False), (ps(b6, 1), T.mB[:], sl(LF, h), False, True, HS, False)], ["mI", "mB", qk, lfs[t]], ["mk" + hs], [b6])
                 V("ts", ["mk" + hs], ["IND" + hs], HS, 1.0, [b6], out=sl(T.IND, h), in0=ps(b6, 1), scalar1=3.5, scalar2=-4.0, op0=OP.is_gt, op1=OP.mult)
-                MM([(ps(b6, 2), T.mI[:], sl(T.Q0, h), True, False, HS, False)] + [(ps(b6, 2), T.mB[:], sl(T["LF_%d" % u], h), False, False, HS, False) for u in range(t + 1)]
-                   + [(ps(b6, 2), T.mI[:], sl(T.IND, h), False, True, HS, False)], ["mI", "mB", "Q0", "IND" + hs] + lfs, ["tt" + hs, "xc" + hs], [b6])
-                A(["tt" + hs], ["th%d_%d" % (t + 1, h)], HS, [b6], out=m0(T["M0_%d" % (t + 1)], h, 2), in_=ps(b6, 2), func=AF.Copy, bias=6.5)
+                MM([(ps(b6, 2), T.mI[:], q0, True, False, HS, False), (ps(b6, 2), T.mB[:], sl(LF, h), False, False, HS, False), (ps(b6, 2), T.mI[:], sl(T.IND, h), False, True, HS, False)],
+                   ["mI", "mB", qk, lfs[t], "IND" + hs], ["tt" + hs, "xc" + hs], [b6])
+                A(["tt" + hs], ["th%d_%d" % (t + 1, h)], HS, [b6], out=m0(T["M0_%d" % (t + 1)], h, 2), in_=ps(b6, 2), func=AF.Copy)
             else:
                 MM([(ps(b6, 1), T.mI[:], sl(T.AB, h), True, False, HS, False)] + [(ps(b6, 1), T.mB[:], sl(T["LF_%d" % u], h), False, u == t, HS, False) for u in range(t + 1)],
                    ["mI", "mB", "AB"] + lfs, ["mk" + hs], [b6])
@@ -479,7 +500,7 @@ def depend(ops):
     return deps
 
 
-BIAS = {}
+BIAS = {'SYG1': -7000, 'Gsnd0': -8000, 'Gsnd1': -8000, 'VSC0': 40000, 'VSC1': 20000, 'VX1': 20000, 'VX0': 20000, 'SG1': -4000, 'VXD0': 20000, 'VMA0': -1000, 'Sw0': 23000, 'SIW0': 17000, 'SIW1': 17000, 'VN0': 2000, 'VN1': 1000, 'SABS0': -2000, 'SABS1': -2000, 'VASH0': 1000, 'VH0': 3000, 'VTMP0': 6000, 'Tkey1': -2000, 'VTJ0': 20000, 'VTJ1': 20000, 'YFIN0': 8000, 'YFIN1': 8000, 'SG0': -3000, 'VXG0': 1000, 'VKT1': 1000, 'VMK0': 8000, 'VMK1': 8000, 'VMA1': 1000, 'Tmk0': -2000, 'Tmk1': -1000, 'SRs0': 8000, 'VTI1': 1000, 'VmKC0': 8000, 'VmKC1': 8000, 'Twc0': 3000, 'VDSC0': 1000, 'VcKC0': 20000, 'VcKC1': 20000, 'VCNT0': -1000, 'VCNT1': -1000, 'NLF0': -17000, 'NLF1': -20000, 'Tq1': -3000, 'Tq0': -3000, 'SE0': -20000, 'Sw1': -6000, 'NLN1': -1000, 'SYG0': -2000, 'Vx0p1': 3000, 'Vx0p0': 3000, 'VmI0': 3000, 'VmI1': 3000, 'Tkey0': 1000, 'STH1': -12000, 'STH0': -9000, 'VOF1': -1000, 'Tring0': -2000, 'VDSC1': 3000, 'VHM0': 20000, 'VK1': -3000, 'SRq0': 48000, 'SX0': -20000, 'SX1': -20000, 'VUND0': -1000, 'VUND1': -1000, 'VIND0': 1000, 'VKT0': 20000, 'SOR1': -20000, 'SOR0': -20000, 'Tring1': -1000, 'SRq1': 28000, 'VKK1': 20000, 'VHM1': -3000, 'GIMK0': -8000, 'VTMP1': 9000, 'VHK0': 20000, 'VHK1': 20000, 'Tt0': 20000, 'Tt1': 20000, 'VLA1': 22000, 'SEA1': 1000, 'GCII0': 8000, 'VLA0': 2000, 'Vbias0': 8000, 'VDMW1': 3000, 'VcPm0': 8000, 'VcPm1': 8000, 'VKAP1': 3000, 'Vc16P0': -1000, 'Vc16P1': -1000, 'VFF0': 3000, 'VYU0': -1000}
 
 
 def klass(o):

import math
from concourse.mybir import AluOpType as OP, ActivationFunctionType as AF

N = 4
DIST = [1, 2, 3, 1]
RO = len(DIST)
S = 256
W = 4096
NH = 2
HS = S // NH
LN2 = math.log(2.0)
WT = 85
CFG = {"npc": 4,
       "vc": ((0, 3),),
       "vc0": ((0, 3),),
       "vh": (),
       "ns": (4, 4),
       "es": (1, 1),
       "nq": (1, 1),
       "bitV": (1, 1), "alpha": 20.0, "win": 300.0,
       "bonus": 1500.0, "g": 1.5, "f": 1.2, "ov": 12.0, "wake": 120.0, "hop": 2000.0}

SCRATCH = {}
for _n, _s, _d in [
    ("X", [128, W], "bfloat16"), ("ASI", [128, W], "int32"), ("ASH", [128, W], "float32"),
    ("XG", [128, W], "bfloat16"), ("YG", [128, W], "bfloat16"), ("DW", [128, W], "bfloat16"), ("E", [128, W], "bfloat16"), ("G", [128, W], "bfloat16"),
    ("CIN", [128, S], "int32"), ("HIN", [128, S], "int32"), ("RIN", [128, S], "int32"), ("FIN", [8, S], "int32"), ("Q8I", [8, S], "int32"),
    ("A8", [8, S], "bfloat16"), ("Q8", [8, S], "bfloat16"), ("AB", [128, S], "bfloat16"), ("IND", [128, S], "bfloat16"),
    ("C", [128, S], "float32"), ("C16", [128, S], "uint16"), ("HK", [128, S], "float32"), ("H16", [128, S], "uint16"),
    ("R", [128, S], "bfloat16"), ("R1", [128, S], "bfloat16"), ("MA", [128, S], "bfloat16"), ("LA", [128, S], "bfloat16"), ("IW", [128, S], "bfloat16"),
    ("AB1", [128, S], "bfloat16"), ("BIT", [128, S], "bfloat16"), ("TI", [128, S], "int32"), ("TJ", [128, S], "int32"), ("KAP", [128, S], "bfloat16"),
    ("CM", [128, S], "float32"), ("KH", [128, S], "float32"), ("HM", [128, S], "float32"), ("UND", [128, S], "bfloat16"), ("DSC", [128, S], "bfloat16"),
    ("XD", [128, S], "bfloat16"), ("YU", [128, S], "bfloat16"), ("KT", [128, S], "float32"), ("SC", [128, S], "float32"),
    ("K32", [128, 16], "int32"), ("N32", [128, 16], "int32"), ("KK", [128, 16], "int32"), ("OF", [128, 16], "int32"), ("OF16", [128, 16], "uint16"),
    ("DM", [128, S], "bfloat16"), ("DMW", [128, S], "bfloat16"), ("TH", [128, S], "float32"),
    ("OC", [128, S], "float32"), ("OH", [128, S], "float32"), ("OR", [128, S], "float32"), ("OA", [128, S], "float32"),
    ("IP", [128, 1], "int32"), ("KI", [128, 1], "int32"), ("B4I", [128, 1], "int32"), ("COL", [128, 16], "float32"), ("COL2", [128, 2], "float32"), ("EA", [128, 1024], "bfloat16"), ("CNH", [128, 1024], "bfloat16"), ("THC", [128, 16], "float32"), ("COLB", [128, 2], "bfloat16"),
    ("IM", [128, 128], "float32"), ("IMG", [128, 128], "float32"), ("IMK", [128, 128], "float32"), ("IMB", [128, 128], "bfloat16"),
    ("SEL", [128, 2048], "bfloat16"), ("CNT", [128, 2048], "bfloat16"),
    ("mB", [128, 128], "bfloat16"), ("mI", [128, 128], "bfloat16"), ("mNI", [128, 128], "bfloat16"), ("mNB", [128, 128], "bfloat16"),
    ("mTB", [128, 128], "bfloat16"), ("mWB", [128, 128], "bfloat16"), ("mCW", [128, 128], "bfloat16"), ("mKC", [128, 128], "bfloat16"),
    ("mNW", [128, 128], "bfloat16"), ("m4", [128, 128], "bfloat16"), ("ONES", [128, 128], "bfloat16"), ("mI2", [128, 128], "bfloat16"), ("TMP", [128, 128], "float32"), ("MK0", [128, 128], "float32"),
    ("fI", [128, 128], "float32"), ("fP", [128, 512], "float32"), ("SD", [128, 128], "float32"), ("CII", [128, 16], "int32"), ("CI", [128, 16], "int32"),
    ("mG8", [8, 128], "bfloat16"),
]:
    SCRATCH[_n] = ("sbuf", _s, _d)
for _t in range(RO):
    SCRATCH["M0_%d" % _t] = ("sbuf", [128, 3 * S], "bfloat16")
    SCRATCH["L0_%d" % _t] = ("sbuf", [128, 3 * S], "bfloat16")
    for _n in ("M1_", "L1_", "FF_", "LF_"):
        SCRATCH[_n + str(_t)] = ("sbuf", [128, S], "bfloat16")
    for _n in ("NS_", "LN_"):
        SCRATCH[_n + str(_t)] = ("sbuf", [128, 16], "uint16")
for _b in range(8):
    SCRATCH["pb%d" % _b] = ("psum", [128, 512], "float32")

SEMAPHORES = ["sT", "sV", "sS", "sG"]
SEMAPHORES += ["ld_%s" % _n for _n in ("x", "ctx", "cand", "pref", "assoc", "fail0")] + ["st_%d" % _i for _i in range(12)]
for _t in range(RO):
    for _m in ("00", "01", "10", "11", "20", "21", "30", "31"):
        SEMAPHORES += ["r%d_%s" % (_t, _m), "l%d_%s" % (_t, _m)]

cP, cK, cG16, cPp, cPm, cS0, cS1, cKC, c16K, cH, c16P = range(11)

_ORDER = {}


PER_ROUND = ("L10", "L11", "L00", "L01", "NS0", "NS1", "LN0", "LN1", "x0_0", "x0_1", "x0p0", "x0p1")


def build(g, T, topo, rank, core):
    ops = []
    cur_t = [0]
    cur_h = [0]
    GR = CFG["g"]

    def key(k):
        return k + "_r%d" % cur_t[0] if k in PER_ROUND else k

    def add(q, fn, rd, wr, cost, banks=(), sem=None, val=1, lat=0.0):
        ops.append({"q": q, "fn": fn, "rd": [key(k) for k in rd], "wr": [key(k) for k in wr], "bk": list(banks), "cost": cost, "sem": sem, "val": val, "lat": lat,
                    "h": cur_h[0], "t": cur_t[0]})

    CY = 0.83 * CFG["f"]

    def vcost(n, rate=1.0):
        return max(64, n * rate) * CY + CFG["ov"]

    def V(name, rd, wr, n, rate=1.0, banks=(), extra=0.0, **kw):
        f = {"tt": g.vector.tensor_tensor, "ts": g.vector.tensor_scalar, "cp": g.vector.tensor_copy, "tr": g.vector.transpose,
             "scan": g.vector.tensor_tensor_scan}[name]
        add("V", lambda: f(**kw), rd, wr, vcost(n, rate) + extra, banks)

    def A(rd, wr, n, banks=(), extra=0.0, rate=1.0, **kw):
        add("S", lambda: g.scalar.activation(**kw), rd, wr, n * rate * CY + 20 + extra, banks)

    def MM(lst, rd, wr, banks):
        def fn():
            ins = None
            for o, l, r, a, b, n, f in lst:
                ins = g.tensor.matmul(out=o, lhsT=l, rhs=r, start=a, stop=b)
            return ins
        add("T", fn, rd, wr, sum(max(64, n) * (4 if f else 1) * 0.42 * 1.22 for o, l, r, a, b, n, f in lst) + 20, banks)

    def col(i):
        return T.COL[:, i:i + 1]

    def sl(b, h):
        return b[:, h * HS:(h + 1) * HS]

    def m0(b, h, j):
        return b[:, (3 * h + j) * HS:(3 * h + j + 1) * HS]

    def ps(b, r):
        return T["pb%d" % b][:, r * 128:(r + 1) * 128]

    def ldw(q, semn, key, dst, src, lat):
        e = g.sync if q == "Y" else g.scalar
        add(q, lambda: e.dma_start(out=dst, in_=src), [], [key], 60, sem="ld_" + semn, val=16, lat=lat)

    ldw("Y", "ctx", "CIN", T.CIN[:], T.ctx[:], 2200)
    ldw("S", "x", "X", T.X[:], T.x[:], 4500)
    ldw("Y", "pref", "RIN", T.RIN[:], T.pref[:], 2300)
    ldw("Y", "cand", "HIN", T.HIN[:], T.cand[:], 2400)
    ldw("Y", "fail0", "FIN", T.FIN[:], T.fail0[:], 2400)
    ldw("S", "assoc", "ASI", T.ASI[:], T.assoc[:], 6500)
    ops[-1]["rd"] = ["X"]

    def iota(dst, key, pattern, base, cm, n, flag=True):
        if flag:
            fn = lambda: g.iota(dst, pattern, base, cm, allow_small_or_imprecise_dtypes=True)
        else:
            fn = lambda: g.iota(dst, pattern, base, cm)
        add("G", fn, [], [key], 130 + 2 * n * CY)

    iota(T.IP[:], "IP", [[1, 1]], 0, 1, 1, False)
    iota(T.IM[:], "IM", [[1, 128]], 0, 0, 128)
    iota(T.IMG[:], "IMG", [[16, 8], [0, 16]], 0, 0, 128)
    iota(T.IMB[:], "IMB", [[1, 128]], 0, 0, 128)
    iota(T.IMK[:], "IMK", [[0, 8], [1, 16]], 0, 0, 128)
    iota(T.CII[:], "CII", [[256, 16]], 15, 0, 16, False)

    V("cp", ["CIN"], ["C160", "C161"], S, out=T.C16[:], in_=T.CIN[:])

    V("ts", ["IP"], ["KI"], 1, out=T.KI[:], in0=T.IP[:], scalar1=15, scalar2=None, op0=OP.bitwise_and)
    V("cp", ["IP"], ["cP"], 1, out=col(cP), in_=T.IP[:])
    V("cp", ["KI"], ["cK"], 1, out=col(cK), in_=T.KI[:])
    V("tt", ["cP", "cK"], ["cG16"], 1, out=col(cG16), in0=col(cP), in1=col(cK), op=OP.subtract)

    def mat(dst, key, src, skey, c, ckey, n=128, rate=1.0):
        V("ts", [skey, ckey], [key], n, rate, out=dst, in0=src, scalar1=c, scalar2=None, op0=OP.is_equal)

    mat(T.mI[:], "mI", T.IM[:], "IM", col(cP), "cP")
    V("ts", ["mI"], ["mNI"], 128, 0.5, out=T.mNI[:], in0=T.mI[:], scalar1=-1.0, scalar2=None, op0=OP.mult)

    def scol(i, key, src, skey, **kw):
        V("ts", [skey], [key], 1, out=col(i), in0=src, **kw)

    def state_from_pref():
        V("cp", ["RIN"], ["R0", "R1_"], S, out=T.R[:], in_=T.RIN[:])
    state_from_pref()
    ops[-1]["wr"] = ["Rs0", "Rs1"]

    def orders(h, t, src, rd, banks=()):
        A(rd, ["w%d_%d" % (t, h)], HS, banks, out=m0(T["M0_%d" % t], h, 1), in_=src, func=AF.Exp, bias=col(12), scale=-11.0 * LN2)
        ops[-1]["rd"].append("bias")
        A(rd, ["IW%d" % h], HS, banks, out=sl(T.IW, h), in_=src, func=AF.Exp, scale=LN2)

    add("V", lambda: g.vector.memset(col(12), WT * LN2), [], ["bias"], 80)
    add("V", lambda: g.vector.memset(col(13), 6.5 * 2.0 ** 96), [], ["bias"], 80)
    add("V", lambda: g.vector.memset(col(14), 15.0 * LN2), [], ["bias"], 80)
    for h in range(NH):
        orders(h, 0, sl(T.R, h), ["Rs%d" % h])

    for k in range(16):
        V("ts", ["IMB", "cG16"], ["SEL%d" % (k // 4)], 128, 0.5, out=T.SEL[:, k * 128:(k + 1) * 128], in0=T.IMB[:], scalar1=float(k), scalar2=col(cG16), op0=OP.subtract, op1=OP.is_equal)
    for j in range(4):
        MM([(T["pb%d" % j][:, 0:512], T.mI[:], T.SEL[:, j * 512:(j + 1) * 512], True, True, 512, False)], ["mI", "SEL%d" % j], ["ring%d" % j], [j])
        m = 512 if j < 3 else 384
        V("tt", ["SEL%d" % j, "SEL%d" % min(j + 1, 3), "ring%d" % j], ["CNT%d" % j], m, 1.0, [j], out=T.CNT[:, j * 512:j * 512 + m], in0=T["pb%d" % j][:, 0:m], in1=T.SEL[:, j * 512 + 128:j * 512 + 128 + m], op=OP.subtract)
    V("cp", ["SEL3"], ["CNT3"], 128, 0.5, out=T.CNT[:, 1920:2048], in_=T.SEL[:, 1920:2048])
    ns = CFG["ns"]
    nx = max(ns)
    allcnt = ["CNT%d" % j for j in range(4)]
    allsel = ["SEL%d" % j for j in range(4)]
    V("ts", allcnt, ["CNH"], 128 * nx, 0.5, out=T.CNH[:, 0:128 * nx], in0=T.CNT[:, 128 * (16 - nx):], scalar1=0.5, scalar2=None, op0=OP.mult)
    for h in range(NH):
        V("ts", ["cK"], ["c8%d" % h], 1, out=T.COL2[:, h:h + 1], in0=col(cK), scalar1=float(16 - ns[h]), scalar2=8.0, op0=OP.is_equal, op1=OP.mult)
    for r in range(16 - nx, 16):
        add("V", lambda r=r: g.vector.memset(T.THC[:, r:r + 1], -0.6 * 2.0 ** (WT - 11 * r)), [], ["thr%d" % r], 65)

    def cntm(r, h):
        if r >= 16 - ns[h]:
            return T.CNH[:, 128 * (r - 16 + nx):128 * (r - 15 + nx)]
        return T.CNT[:, 128 * r:128 * (r + 1)]
    mat(T.mB[:], "mB", T.IMG[:], "IMG", col(cG16), "cG16")
    add("V", lambda: g.vector.memset(T.ONES[:], 1.0), [], ["ONES"], 80)
    A(["cK", "bias"], ["cb2"], 1, out=T.COLB[:, 0:1], in_=col(cK), func=AF.Exp, bias=col(14), scale=-LN2)
    A(["cK", "bias"], ["cbw"], 1, out=T.COLB[:, 1:2], in_=col(cK), func=AF.Exp, bias=col(12), scale=-11.0 * LN2)
    V("ts", ["mB", "cb2"], ["mWB"], 128, 1.0, out=T.mWB[:], in0=T.mB[:], scalar1=T.COLB[:, 0:1], scalar2=None, op0=OP.mult)
    V("ts", ["mWB"], ["mNW"], 128, 0.5, out=T.mNW[:], in0=T.mWB[:], scalar1=-1.0, scalar2=None, op0=OP.mult)
    V("ts", ["mI"], ["m4"], 128, 0.5, out=T.m4[:], in0=T.mI[:], scalar1=-4.0, scalar2=None, op0=OP.mult)
    V("cp", ["HIN"], ["H160", "H161"], S, out=T.H16[:], in_=T.HIN[:])
    V("ts", ["mB", "cbw"], ["TMP"], 128, 1.0, out=T.TMP[:], in0=T.mB[:], scalar1=T.COLB[:, 1:2], scalar2=-0.6, op0=OP.mult, op1=OP.mult)
    V("ts", ["IMK"], ["MK0"], 128, 1.0, out=T.MK0[:], in0=T.IMK[:], scalar1=0.5, scalar2=None, op0=OP.is_gt)
    V("tt", ["TMP", "MK0"], ["mCW"], 128, 2.0, out=T.mCW[:], in0=T.TMP[:], in1=T.MK0[:], op=OP.mult)
    scol(cKC, "cKC", col(cK), "cK", scalar1=0.0, scalar2=-(2.0 ** -90), op0=OP.is_equal, op1=OP.add)
    V("ts", ["mI", "cKC"], ["mKC"], 128, 1.0, out=T.mKC[:], in0=T.mI[:], scalar1=col(cKC), scalar2=None, op0=OP.mult)
    mat(T.fI[:], "fI", T.IM[:], "IM", col(cP), "cP")
    V("cp", ["CIN"], ["Cs0", "Cs1"], S, out=T.C[:], in_=T.CIN[:])
    scol(cH, "cH", col(cK), "cK", scalar1=-4096.0, scalar2=61440.0, op0=OP.mult, op1=OP.add)
    V("ts", ["HIN", "cH"], ["HK0", "HK1"], S, out=T.HK[:], in0=T.HIN[:], scalar1=col(cH), scalar2=2.0 ** -17, op0=OP.add, op1=OP.mult)
    V("ts", ["mB"], ["mNB"], 128, 0.5, out=T.mNB[:], in0=T.mB[:], scalar1=-1.0, scalar2=None, op0=OP.mult)
    V("ts", ["mI"], ["mI2"], 128, 0.5, out=T.mI2[:], in0=T.mI[:], scalar1=2.0, scalar2=None, op0=OP.mult)
    V("tt", ["mI2", "mB"], ["mTB"], 128, 2.0, out=T.mTB[:], in0=T.mI2[:], in1=T.mB[:], op=OP.subtract)
    V("ts", ["IP"], ["B4I"], 1, out=T.B4I[:], in0=T.IP[:], scalar1=4, scalar2=1, op0=OP.arith_shift_right, op1=OP.bitwise_and)
    V("cp", ["B4I"], ["cS1"], 1, out=col(cS1), in_=T.B4I[:])
    scol(cS0, "cS0", col(cS1), "cS1", scalar1=-1.0, scalar2=1.0, op0=OP.mult, op1=OP.add)
    scol(cPp, "cPp", col(cP), "cP", scalar1=16.0, scalar2=None, op0=OP.add)
    scol(cPm, "cPm", col(cP), "cP", scalar1=-16.0, scalar2=None, op0=OP.add)
    scol(c16K, "c16K", col(cK), "cK", scalar1=16.0, scalar2=None, op0=OP.mult)
    scol(c16P, "c16P", col(cP), "cP", scalar1=16.0, scalar2=None, op0=OP.mult)
    for j, (c, ck, s, sk) in enumerate([(cP, "cP", cS0, "cS0"), (cPp, "cPp", cS0, "cS0"), (cPm, "cPm", cS1, "cS1"), (cP, "cP", cS1, "cS1")]):
        V("ts", ["IM", ck, sk], ["fP"], 128, 1.0, out=T.fP[:, j * 128:(j + 1) * 128], in0=T.IM[:], scalar1=col(c), scalar2=col(s), op0=OP.is_equal, op1=OP.mult)
    V("ts", ["IMK"], ["SD"], 128, 1.0, out=T.SD[:], in0=T.IMK[:], scalar1=0.0, scalar2=-4096.0, op0=OP.is_equal, op1=OP.mult)
    V("ts", ["CII", "c16K"], ["CI"], 16, 1.0, out=T.CI[:], in0=T.CII[:], scalar1=col(c16K), scalar2=None, op0=OP.add)
    V("ts", ["IMG", "c16P"], ["mG8"], 128, 1.0, out=T.mG8[:], in0=T.IMG[0:8, :], scalar1=T.COL[0:8, c16P:c16P + 1], scalar2=None, op0=OP.is_equal)
    V("cp", ["FIN"], ["A8"], S, out=T.A8[:], in_=T.FIN[:])
    V("ts", ["FIN"], ["Q8I"], S, out=T.Q8I[:], in0=T.FIN[:], scalar1=3, scalar2=None, op0=OP.bitwise_and)
    V("cp", ["Q8I"], ["Q8"], S, out=T.Q8[:], in_=T.Q8I[:])
    MM([(T.pb6[:, 0:256], T.mG8[:], T.A8[:], True, True, S, False), (T.pb6[:, 256:512], T.mG8[:], T.Q8[:], True, True, S, False)],
       ["mG8", "A8", "Q8"], ["b6a"], [6])
    A(["b6a"], ["AB"], S, [6], out=T.AB[:], in_=T.pb6[:, 0:256], func=AF.Copy)
    for h in range(NH):
        A(["b6a"], ["th0_%d" % h], HS, [6], out=m0(T.M0_0, h, 2), in_=T.pb6[:, 256 + h * HS:256 + (h + 1) * HS], func=AF.Copy)

    for j in range(8):
        V("ts", ["ASI", "cH"], ["ASH"], W // 8, 1.0, out=T.ASH[:, j * 512:(j + 1) * 512], in0=T.ASI[:, j * 512:(j + 1) * 512],
          scalar1=col(cH), scalar2=2.0 ** -17, op0=OP.add, op1=OP.mult)

    def send(t, m, dst, src_ap, dst_ap, rd, wr, lat):
        rid, pid, _s = topo.addr(dst)
        mask = topo.mask(core, dst)
        ne = len(topo.engines(core, dst))
        rs, ls = "r%d_%s" % (t, m), "l%d_%s" % (t, m)
        add("G", lambda: g.remote_dma(out_ap=dst_ap, in_ap=src_ap, remote_sem=T.sem[rs], local_sem=T.sem[ls], pid=pid, routing_id=rid, dma_engine_mask=mask),
            rd, [], 700)
        ops[-1]["remote"] = (ls, ne)
        k = len(ops) - 1
        add("N", None, [], wr, 0, sem=rs, val=ne, lat=lat)
        ops[-1]["after"] = k

    def gather(t, h, src16, dst, key, okey, vp):
        npc = CFG["npc"]
        step = HS // npc
        for j in range(npc):
            a = h * HS + j * step
            offs = src16[:, a:a + step]
            o = dst[:, 16 * a:16 * (a + step)]
            n = 16 * step
            if (h, j) in vp:
                V("cp", ["X", okey + str(h)], [key + "%d%d" % (h, j)], n, GR, out=o, in_=T.X[:].indirect(offs))
            else:
                A(["X", okey + str(h)], [key + "%d%d" % (h, j)], n, (), 45, GR, out=o, in_=T.X[:].indirect(offs), func=AF.Copy)

    ring = [0]

    for t in range(RO):
        hear = T.cores[(rank + DIST[t]) % N]
        spk = T.cores[(rank - DIST[t]) % N]
        M0, L0 = T["M0_%d" % t], T["L0_%d" % t]
        M1, L1 = T["M1_%d" % t], T["L1_%d" % t]
        NS, LN = T["NS_%d" % t], T["LN_%d" % t]
        FF, LF = T["FF_%d" % t], T["LF_%d" % t]
        last = t == RO - 1
        cur_t[0] = t
        for h in range(NH):
            hs = str(h)
            cur_h[0] = h
            gather(t, h, T.C16, T.XG, "XG", "C16", CFG["vc"] if t else CFG["vc0"])
            xgk = ["XG%d%d" % (h, j) for j in range(CFG["npc"])]

            b4 = 4 + h
            nq = CFG["nq"][h]
            qs = HS // nq
            npq = CFG["npc"] // nq
            V("cp", xgk, ["x0_%d" % h], HS, 0.5, out=m0(M0, h, 0), in_=T.XG[:, h * 2048:(h + 1) * 2048:16])
            for q in range(nq):
                qk = xgk[q * npq:(q + 1) * npq]

                def xg(k, h=h, q=q, qs=qs):
                    return T.XG[:, h * 2048 + q * qs * 16 + k:h * 2048 + (q + 1) * qs * 16:16]

                def dw(k, h=h, q=q, qs=qs):
                    return T.DW[:, h * 2048 + k * 128 + q * qs:h * 2048 + k * 128 + (q + 1) * qs]
                wq = M0[:, (3 * h + 1) * HS + q * qs:(3 * h + 1) * HS + (q + 1) * qs]
                sk = T["pb%d" % b4][:, q * qs:(q + 1) * qs]
                nk = 512 // qs
                for c in range(16 // nk):
                    ks = range(1 + nk * c, min(16, 1 + nk + nk * c))
                    b = ring[0] % 4
                    ring[0] += 1
                    for s0 in range(0, len(ks), 4):
                        lst = []
                        for j in range(s0, min(s0 + 4, len(ks))):
                            o = T["pb%d" % b][:, j * qs:(j + 1) * qs]
                            lst.append((o, T.mI[:], xg(ks[j]), True, False, qs, False))
                            lst.append((o, T.mNI[:], xg(0), False, True, qs, False))
                        MM(lst, qk + ["mI", "mNI"], ["ring%d" % b], [b])
                    for j, k in enumerate(ks):
                        V("tt", ["ring%d" % b, "w%d_%d" % (t, h)], ["DW%d%d_%d" % (h, q, k)], qs, 1.0, [b],
                          out=dw(k), in0=T["pb%d" % b][:, j * qs:(j + 1) * qs], in1=wq, op=OP.mult)
                    MM([(sk, T.SEL[:, k * 128:(k + 1) * 128], dw(k), k == 1, k == 15, qs, False) for k in ks],
                       allsel + ["DW%d%d_%d" % (h, q, k) for k in ks], ["Sk" + hs], [b4])
            A(["Sk" + hs], ["ABS" + hs], HS, [b4], out=sl(T.AB1, h), in_=ps(b4, 0), func=AF.Abs)

            def G(r, h=h):
                return T.G[:, h * 2048 + r * 128:h * 2048 + (r + 1) * 128]
            for r in range(16):
                if r >= 16 - CFG["ns"][h]:
                    A(["ABS" + hs, "thr%d" % r], ["G%d_%d" % (h, r)], HS, out=G(r), in_=sl(T.AB1, h), func=AF.Sign, bias=T.THC[:, r:r + 1])
                else:
                    V("ts", ["ABS" + hs], ["G%d_%d" % (h, r)], HS, 0.5, out=G(r), in0=sl(T.AB1, h), scalar1=0.6 * 2.0 ** (WT - 11 * r), scalar2=None, op0=OP.is_ge)
                if r % 4 == 3:
                    MM([(ps(b4, 1), cntm(q, h), G(q), q == 0, q == 15, HS, False) for q in range(r - 3, r + 1)],
                       allcnt + ["CNH"] + ["G%d_%d" % (h, q) for q in range(r - 3, r + 1)], ["cnt" + hs], [b4])
            c8 = T.COL2[:, h:h + 1]
            if CFG["bitV"][h]:
                V("ts", ["cnt" + hs, "c8" + hs], ["BIT" + hs], HS, 1.0, [b4], out=sl(T.BIT, h), in0=ps(b4, 1), scalar1=c8, scalar2=0.5, op0=OP.add, op1=OP.is_gt)
            else:
                A(["cnt" + hs, "c8" + hs], ["BIT" + hs], HS, [b4], out=sl(T.BIT, h), in_=ps(b4, 1), func=AF.Sign, bias=c8)
            MM([(ps(b4, 0), T.mWB[:], T.ONES[:], True, False, HS, False), (ps(b4, 0), T.mNW[:], sl(T.BIT, h), False, True, HS, False)],
               ["mNW", "mWB", "ONES", "BIT" + hs], ["Sk" + hs], [b4])
            V("tt", ["Sk" + hs, "IW" + hs], ["TI" + hs], HS, 1.0, [b4], out=sl(T.TI, h), in0=ps(b4, 0), in1=sl(T.IW, h), op=OP.mult)
            V("ts", ["TI" + hs], ["TJ" + hs], HS, 1.0, out=sl(T.TJ, h), in0=sl(T.TI, h), scalar1=32768, scalar2=None, op0=OP.bitwise_and)
            V("tt", ["TJ" + hs, "x0_%d" % h], ["x0p%d" % h], HS, 2.0, out=sl(M1, h), in0=m0(M0, h, 0), in1=sl(T.TJ, h), op=OP.add)
            send(t, "1%d" % h, hear, sl(M1, h), sl(L1, h), ["x0p%d" % h], ["L1" + hs], CFG["hop"])
            MM([(ps(b4, 1), T.mI[:], sl(T.AB1, h), True, False, HS, False), (ps(b4, 1), T.mCW[:], sl(T.BIT, h), False, False, HS, False),
                (ps(b4, 1), T.mKC[:], T.ONES[:], False, True, HS, False)], ["ABS" + hs, "mI", "mCW", "mKC", "ONES", "BIT" + hs], ["cnt" + hs, "dB" + hs], [b4])
            V("ts", ["cnt" + hs], ["KAP" + hs], HS, 1.0, [b4], out=sl(T.KAP, h), in0=ps(b4, 1), scalar1=0.0, scalar2=8192.0, op0=OP.is_gt, op1=OP.mult)
            MM([(ps(b4, 2), T.fI[:], sl(T.C, h), True, False, HS, True), (ps(b4, 2), T.mNI[:], sl(T.KAP, h), False, True, HS, False)],
               ["fI", "mNI", "Cs" + hs, "KAP" + hs], ["q" + hs], [b4])
            send(t, "0%d" % h, hear, M0[:, h * 3 * HS:(h + 1) * 3 * HS], L0[:, h * 3 * HS:(h + 1) * 3 * HS], ["x0_" + hs, "w%d_%d" % (t, h), "th%d_%d" % (t, h)], ["L0" + hs], CFG["hop"] + 200)
        for h in range(NH):
            cur_h[0] = h
            gather(t, h, T.H16, T.YG, "YG", "H16", CFG["vh"])
        for h in range(NH):
            hs = str(h)
            cur_h[0] = h
            ygk = ["YG%d%d" % (h, j) for j in range(CFG["npc"])]
            b6 = 6 + h
            V("ts", ["L1" + hs], ["DSC" + hs], HS, 0.5, out=sl(T.DSC, h), in0=sl(L1, h), scalar1=1000.0, scalar2=None, op0=OP.is_lt)
            lst = [(ps(b6, 3), T.mI[:], m0(L0, h, 1), True, True, HS, False)]
            if not last:
                lst.append((ps(b6, 2), T.mI[:], sl(L1, h), True, True, HS, False))
                V("ts", ["L1" + hs], ["UND" + hs], HS, 0.5, out=sl(T.UND, h), in0=sl(L1, h), scalar1=1000.0, scalar2=None, op0=OP.is_gt)
            MM(lst, ["mI", "L0" + hs, "L1" + hs], ["wc" + hs, "xc" + hs], [b6])
            if not last:
                V("tt", ["xc" + hs, "DSC" + hs], ["XD" + hs], HS, 1.0, [b6], out=sl(T.XD, h), in0=ps(b6, 2), in1=sl(T.DSC, h), op=OP.mult)
            MM([(ps(b6, 0), T.fI[:], sl(T.HK, h), True, False, HS, True), (ps(b6, 0), T.mNB[:], sl(T.DSC, h), False, False, HS, False)],
               ["fI", "mNB", "HK" + hs, "DSC" + hs], ["key" + hs], [b6])
            for c in range(4):
                b = ring[0] % 4
                ring[0] += 1
                ks = range(4 * c, 4 * c + 4)
                byS = c >= 4 - CFG["es"][h]
                lst = []
                for j, k in enumerate(ks):
                    lst.append((ps(b, j), T.mI[:], T.YG[:, h * 2048 + k:(h + 1) * 2048:16], True, not byS, HS, False))
                    if byS:
                        lst.append((ps(b, j), T.mNI[:], sl(L1, h), False, True, HS, False))
                MM(lst, ygk + ["mI"] + (["mNI", "L1" + hs] if byS else []), ["ring%d" % b], [b])
                if byS:
                    A(["ring%d" % b], ["EA" + hs], 512, [b], out=T.EA[:, h * 512:(h + 1) * 512], in_=T["pb%d" % b][:, 0:512], func=AF.Abs)
                    A(["EA" + hs], ["E%d_%d" % (h, k) for k in ks], 512, out=T.E[:, h * 2048 + c * 512:h * 2048 + (c + 1) * 512], in_=T.EA[:, h * 512:(h + 1) * 512],
                      func=AF.Relu, scale=-1.0, bias=1.0)
                for j, k in enumerate(ks if not byS else ()):
                    V("tt", ["ring%d" % b, "L1" + hs], ["E%d_%d" % (h, k)], HS, 1.0, [b],
                      out=T.E[:, h * 2048 + k * 128:h * 2048 + (k + 1) * 128], in0=ps(b, j), in1=sl(L1, h), op=OP.is_equal)
                MM([(ps(b6, 0), T.SEL[:, k * 128:(k + 1) * 128], T.E[:, h * 2048 + k * 128:h * 2048 + (k + 1) * 128], False, k == 15, HS, False) for k in ks],
                   allsel + ["E%d_%d" % (h, k) for k in ks], ["key" + hs], [b6])
            V("tr", ["key" + hs], ["KT" + hs], HS, 1.0, [b6], out=sl(T.KT, h), in_=ps(b6, 0))
            A(["key" + hs], ["KH" + hs], HS, [b6], out=sl(T.KH, h), in_=ps(b6, 0), func=AF.Relu, scale=-1.0)
            V("scan", ["KT" + hs, "SD"], ["SC" + hs], HS, 1.0, out=sl(T.SC, h), data0=T.SD[:], data1=sl(T.KT, h), initial=-4096.0, op0=OP.add, op1=OP.max)
            lst = []
            for hh in range(2):
                for g2 in range(2):
                    lst.append((T["pb%d" % b6][:, 128 + hh:136:2], T.fP[:, (2 * hh + g2) * 128:(2 * hh + g2 + 1) * 128],
                                T.SC[:, h * HS + g2 * 16 + 15:(h + 1) * HS:32], g2 == 0, g2 == 1, 4, True))
            MM(lst, ["fP", "SC" + hs], ["mk" + hs], [b6])
            ws = slice(8 * h, 8 * h + 8)
            V("ts", ["mk" + hs], ["K32" + hs], 8, 1.0, [b6], out=T.K32[:, ws], in0=T["pb%d" % b6][:, 128:136], scalar1=131072.0, scalar2=None, op0=OP.mult)
            V("ts", ["K32" + hs], ["N32" + hs], 8, out=T.N32[:, ws], in0=T.K32[:, ws], scalar1=4095, scalar2=None, op0=OP.bitwise_and)
            V("cp", ["N32" + hs], ["NS" + hs], 8, out=NS[:, ws], in_=T.N32[:, ws])
            send(t, "2%d" % h, spk, NS[:, ws], LN[:, ws], ["NS" + hs], ["LN" + hs], CFG["hop"] - 100)
            V("ts", ["K32" + hs], ["KK" + hs], 8, out=T.KK[:, ws], in0=T.K32[:, ws], scalar1=12, scalar2=15, op0=OP.arith_shift_right, op1=OP.bitwise_and)
            V("tt", ["KK" + hs, "CI"], ["OF" + hs], 8, out=T.OF[:, ws], in0=T.CI[:, 0:8], in1=T.KK[:, ws], op=OP.subtract)
            V("cp", ["OF" + hs], ["OF16" + hs], 8, out=T.OF16[:, ws], in_=T.OF[:, ws])
            ysrc = T.YG[:, h * 2048:(h + 1) * 2048].indirect(T.OF16[:, ws])
            if not last:
                V("tt", ygk + ["OF16" + hs, "UND" + hs], ["YU" + hs], HS, GR, (), 40, out=sl(T.YU, h), in0=ysrc, in1=sl(T.UND, h), op=OP.mult)
            V("tt", ygk + ["OF16" + hs, "L0" + hs], ["DM" + hs], HS, GR, (), 40, out=sl(T.DM, h), in0=ysrc, in1=m0(L0, h, 0), op=OP.not_equal)
            V("tt", ["wc" + hs, "DM" + hs], ["DMW" + hs], HS, 1.0, [b6], out=sl(T.DMW, h), in0=ps(b6, 3), in1=sl(T.DM, h), op=OP.mult)
            MM([(ps(b6, 2), T.mNB[:], sl(T.DM, h), True, False, HS, False), (ps(b6, 2), T.mI[:], m0(L0, h, 2), False, True, HS, False),
                (ps(b6, 3), T.mTB[:], sl(T.DMW, h), True, True, HS, False)], ["mNB", "mI", "mTB", "DM" + hs, "DMW" + hs, "L0" + hs], ["tt" + hs, "wc" + hs, "xc" + hs], [b6])
            A(["tt" + hs, "bias"], ["TH" + hs], HS, [b6], out=sl(T.TH, h), in_=ps(b6, 2), func=AF.Relu, scale=2.0 ** 96, bias=col(13))
            V("tt", ["tt" + hs, "TH" + hs], ["FF%d_%d" % (t, h)], HS, 1.0, [b6], out=sl(FF, h), in0=ps(b6, 3), in1=sl(T.TH, h), op=OP.is_gt)
            send(t, "3%d" % h, spk, sl(FF, h), sl(LF, h), ["FF%d_%d" % (t, h)], ["LF%d_%d" % (t, h)], CFG["hop"])
        if not last:
            for h in range(NH):
                hs = str(h)
                cur_h[0] = h
                V("tt", ["YU" + hs, "XD" + hs, "OF16" + hs], ["X"], HS, 3.5, (), 40, out=T.X[:, h * 2048:(h + 1) * 2048].indirect(T.OF16[:, 8 * h:8 * h + 8]),
                  in0=sl(T.YU, h), in1=sl(T.XD, h), op=OP.add)
        for h in range(NH):
            hs = str(h)
            cur_h[0] = h
            b4, b6 = 4 + h, 6 + h
            ws = slice(8 * h, 8 * h + 8)
            V("tt", ["ASI", "LN" + hs, "KAP" + hs], ["CM" + hs], HS, 1.5, (), 40, out=sl(T.CM, h), in0=T.ASI[:].indirect(LN[:, ws]), in1=sl(T.KAP, h), op=OP.min)
            V("tt", ["CM" + hs, "q" + hs], ["Cs" + hs], HS, 1.0, [b4], out=sl(T.C, h), in0=ps(b4, 2), in1=sl(T.CM, h), op=OP.max)
            if not last:
                V("cp", ["Cs" + hs], ["C16" + hs], HS, 1.0, out=sl(T.C16, h), in_=sl(T.C, h))
            V("tt", ["ASH", "NS" + hs, "KH" + hs], ["HM" + hs], HS, 1.5, (), 40, out=sl(T.HM, h), in0=T.ASH[:].indirect(NS[:, ws]), in1=sl(T.KH, h), op=OP.min)
            V("tt", ["HM" + hs, "key" + hs], ["HK" + hs], HS, 1.0, [b6], out=sl(T.HK, h), in0=ps(b6, 0), in1=sl(T.HM, h), op=OP.max)
            if not last:
                V("ts", ["HK" + hs, "cH"], ["H16" + hs], HS, 1.0, out=sl(T.H16, h), in0=sl(T.HK, h), scalar1=131072.0, scalar2=col(cH), op0=OP.mult, op1=OP.subtract)
            else:
                V("ts", ["HK" + hs, "cH"], ["OH" + hs], HS, 1.0, out=sl(T.OH, h), in0=sl(T.HK, h), scalar1=131072.0, scalar2=col(cH), op0=OP.mult, op1=OP.subtract)
            if t == 0:
                MM([(ps(b4, 3), T.mI[:], sl(T.R, h), True, True, HS, False)], ["mI", "Rs" + hs], ["t2" + hs], [b4])
            cur, ck, pc, pk = T.R, "Rs" + hs, 3, "t2" + hs
            for role, (f, fk) in enumerate([(LF, "LF%d_%d" % (t, h)), (FF, "FF%d_%d" % (t, h))]):
                V("tt", [pk, fk], ["MA" + hs], HS, 1.0, [b4], out=sl(T.MA, h), in0=ps(b4, pc), in1=sl(f, h), op=OP.mult)
                MM([(ps(b4, 1), T.mB[:], sl(T.MA, h), True, True, HS, False)], ["mB", "MA" + hs], ["cnt" + hs, "dB" + hs], [b4])
                V("tt", [ck, "cnt" + hs], ["LA" + hs], HS, 1.0, [b4], out=sl(T.LA, h), in0=ps(b4, 1), in1=sl(cur, h), op=OP.is_gt)
                nc, nk = (2, "q" + hs) if role == 0 else (3, "t2" + hs)
                MM([(ps(b4, nc), T.mI[:], sl(cur, h), True, False, HS, False), (ps(b4, nc), T.mNI[:], sl(T.MA, h), False, False, HS, False),
                    (ps(b4, nc), T.mI[:], sl(T.LA, h), False, True, HS, False)], ["mI", "mNI", ck, "MA" + hs, "LA" + hs], [nk], [b4])
                if role == 0:
                    A([nk], ["Rq" + hs], HS, [b4], out=sl(T.R1, h), in_=ps(b4, nc), func=AF.Copy)
                    cur, ck = T.R1, "Rq" + hs
                elif not last:
                    orders(h, t + 1, ps(b4, nc), [nk], [b4])
                    A([nk], ["Rs" + hs], HS, [b4], out=sl(T.R, h), in_=ps(b4, nc), func=AF.Copy)
                else:
                    A([nk], ["OR" + hs], HS, [b4], out=sl(T.OR, h), in_=ps(b4, nc), func=AF.Copy)
                pc, pk = nc, nk
            lfs = ["LF%d_%d" % (u, h) for u in range(t + 1)]
            if not last:
                q0, qk = m0(M0, h, 2), "th%d_%d" % (t, h)
                MM([(ps(b6, 1), T.mI[:], q0, True, False, HS, False), (ps(b6, 1), T.mB[:], sl(LF, h), False, True, HS, False)], ["mI", "mB", qk, lfs[t]], ["mk" + hs], [b6])
                V("ts", ["mk" + hs], ["IND" + hs], HS, 1.0, [b6], out=sl(T.IND, h), in0=ps(b6, 1), scalar1=3.5, scalar2=-4.0, op0=OP.is_gt, op1=OP.mult)
                MM([(ps(b6, 2), T.mI[:], q0, True, False, HS, False), (ps(b6, 2), T.mB[:], sl(LF, h), False, False, HS, False), (ps(b6, 2), T.mI[:], sl(T.IND, h), False, True, HS, False)],
                   ["mI", "mB", qk, lfs[t], "IND" + hs], ["tt" + hs, "xc" + hs], [b6])
                A(["tt" + hs], ["th%d_%d" % (t + 1, h)], HS, [b6], out=m0(T["M0_%d" % (t + 1)], h, 2), in_=ps(b6, 2), func=AF.Copy)
            else:
                MM([(ps(b6, 1), T.mI[:], sl(T.AB, h), True, False, HS, False)] + [(ps(b6, 1), T.mB[:], sl(T["LF_%d" % u], h), False, u == t, HS, False) for u in range(t + 1)],
                   ["mI", "mB", "AB"] + lfs, ["mk" + hs], [b6])
                A(["mk" + hs], ["OA" + hs], HS, [b6], out=sl(T.OA, h), in_=ps(b6, 1), func=AF.Copy)

    def store(i, q, dst, src, rd):
        e = g.sync if q == "Y" else g.scalar
        add(q, lambda: e.dma_start(out=dst, in_=src), rd, ["out%d" % i], 60, sem="st_%d" % i, val=16, lat=2000)
    for h in range(NH):
        store(h, "Y", sl(T.yctx, h), sl(T.C, h), ["Cs%d" % h])
        store(2 + h, "Y", sl(T.ycand, h), sl(T.OH, h), ["OH%d" % h])
        store(4 + h, "Y", sl(T.ypref, h), sl(T.OR, h), ["OR%d" % h])
        store(6 + h, "Y", sl(T.yfail, h), T.OA[0:128:16, h * HS:(h + 1) * HS], ["OA%d" % h])
    return ops


def depend(ops):
    lastw, readers, lastb = {}, {}, {}
    deps = []
    for i, o in enumerate(ops):
        d = {}
        for k in o["rd"]:
            for w in lastw.get(k, ()):
                d[w] = True
        for k in o["wr"]:
            for w in lastw.get(k, ()):
                d[w] = True
            for r in readers.get(k, ()):
                if r != i:
                    d[r] = True
        for b in o["bk"]:
            if b in lastb:
                d.setdefault(lastb[b], False)
        if "after" in o:
            d[o["after"]] = True
        deps.append(d)
        for k in o["rd"]:
            readers.setdefault(k, []).append(i)
        for k in o["wr"]:
            lastw[k] = [i]
            readers[k] = []
        for b in o["bk"]:
            lastb[b] = i
    return deps


BIAS = {'SYG1': -7000, 'Gsnd0': -8000, 'Gsnd1': -8000, 'VSC0': 40000, 'VSC1': 20000, 'VX1': 20000, 'VX0': 20000, 'SG1': -4000, 'VXD0': 20000, 'VMA0': -1000, 'Sw0': 23000, 'SIW0': 17000, 'SIW1': 17000, 'VN0': 2000, 'VN1': 1000, 'SABS0': -2000, 'SABS1': -2000, 'VASH0': 1000, 'VH0': 3000, 'VTMP0': 6000, 'Tkey1': -2000, 'VTJ0': 20000, 'VTJ1': 20000, 'YFIN0': 8000, 'YFIN1': 8000, 'SG0': -3000, 'VXG0': 1000, 'VKT1': 1000, 'VMK0': 8000, 'VMK1': 8000, 'VMA1': 1000, 'Tmk0': -2000, 'Tmk1': -1000, 'SRs0': 8000, 'VTI1': 1000, 'VmKC0': 8000, 'VmKC1': 8000, 'Twc0': 3000, 'VDSC0': 1000, 'VcKC0': 20000, 'VcKC1': 20000, 'VCNT0': -1000, 'VCNT1': -1000, 'NLF0': -17000, 'NLF1': -20000, 'Tq1': -3000, 'Tq0': -3000, 'SE0': -20000, 'Sw1': -6000, 'NLN1': -1000, 'SYG0': -2000, 'Vx0p1': 3000, 'Vx0p0': 3000, 'VmI0': 3000, 'VmI1': 3000, 'Tkey0': 1000, 'STH1': -12000, 'STH0': -9000, 'VOF1': -1000, 'Tring0': -2000, 'VDSC1': 3000, 'VHM0': 20000, 'VK1': -3000, 'SRq0': 48000, 'SX0': -20000, 'SX1': -20000, 'VUND0': -1000, 'VUND1': -1000, 'VIND0': 1000, 'VKT0': 20000, 'SOR1': -20000, 'SOR0': -20000, 'Tring1': -1000, 'SRq1': 28000, 'VKK1': 20000, 'VHM1': -3000, 'GIMK0': -8000, 'VTMP1': 9000, 'VHK0': 20000, 'VHK1': 20000, 'Tt0': 20000, 'Tt1': 20000, 'VLA1': 22000, 'SEA1': 1000, 'GCII0': 8000, 'VLA0': 2000, 'Vbias0': 8000, 'VDMW1': 3000, 'VcPm0': 8000, 'VcPm1': 8000, 'VKAP1': 3000, 'Vc16P0': -1000, 'Vc16P1': -1000, 'VFF0': 3000, 'VYU0': -1000}


def klass(o):
    w = o["wr"][0] if o["wr"] else "snd" + o["remote"][0].split("_")[1][0]
    a = w.split("_")[0]
    while a and a[-1].isdigit():
        a = a[:-1]
    return "%s%s%d" % (o["q"], a, o["h"])


def schedule(ops, deps):
    n = len(ops)
    succ = [[] for _ in range(n)]
    for i, d in enumerate(deps):
        for j in d:
            succ[j].append(i)
    WAKE, alpha, win = CFG["wake"], CFG["alpha"], CFG["win"]
    prio = [0.0] * n
    for i in range(n - 1, -1, -1):
        m = 0.0
        for j in succ[i]:
            m = max(m, prio[j] + (WAKE if ops[j]["q"] != ops[i]["q"] else 30.0))
        prio[i] = m + ops[i]["cost"] + ops[i]["lat"]
    for i in range(n):
        if ops[i]["h"] == 0:
            prio[i] += CFG["bonus"]
        prio[i] += BIAS.get(klass(ops[i]), 0.0)
    left = [len(d) for d in deps]
    ready = [0.0] * n
    fin = [0.0] * n
    beg = [0.0] * n
    avail = {}
    free = {}
    for i in range(n):
        avail.setdefault(ops[i]["q"], [])
        free.setdefault(ops[i]["q"], 0.0)
        if left[i] == 0:
            avail[ops[i]["q"]].append(i)
    order = []
    while True:
        best = None
        for q in avail:
            if not avail[q]:
                continue
            fq = free[q] if q != "N" else 0.0
            est = min(max(fq, ready[i]) for i in avail[q])
            i, top = None, None
            for z in avail[q]:
                zs = max(fq, ready[z])
                if zs <= est + win:
                    sc = prio[z] - alpha * (zs - est)
                    if top is None or sc > top:
                        i, top = z, sc
            st = max(fq, ready[i])
            if best is None or st < best[0]:
                best = (st, i, q)
        if best is None:
            break
        st, i, q = best
        avail[q].remove(i)
        order.append(i)
        beg[i] = st
        free[q] = st + ops[i]["cost"]
        fin[i] = st + ops[i]["cost"] + ops[i]["lat"]
        for j in succ[i]:
            ready[j] = max(ready[j], fin[i] + (WAKE if ops[j]["q"] != q else (30.0 if deps[j][i] else 0.0)))
            left[j] -= 1
            if left[j] == 0:
                avail[ops[j]["q"]].append(j)
    return order, beg, fin


def rank_program(g, core, T, topo):
    rank = T.rank_of(core)
    if rank is None:
        return
    ops = build(g, T, topo, rank, core)
    deps = depend(ops)
    if "o" not in _ORDER:
        _ORDER["o"] = schedule(ops, deps)[0]
    order = _ORDER["o"]
    eng = {"V": g.vector, "S": g.scalar, "T": g.tensor, "G": g, "Y": g.sync}
    cnt = {}
    done = {}
    clock = {}
    know = {q: {} for q in "VSTGY"}
    for i in order:
        o = ops[i]
        q = o["q"]
        if q == "N":
            done[i] = (o["sem"], o["val"])
            clock[i] = {o["sem"]: o["val"]}
            cnt[o["sem"]] = o["val"]
            continue
        need = {}
        for d, raw in deps[i].items():
            od = ops[d]
            if od["q"] == q and od["sem"] is None and (not raw or q in "TG"):
                if not (q == "G"):
                    continue
                continue
            s, v = done[d]
            if know[q].get(s, 0) < v and (s not in need or need[s][0] < v):
                need[s] = (v, d)
        for s in list(need):
            v, d = need[s]
            for s2 in need:
                if s2 != s and clock[need[s2][1]].get(s, 0) >= v:
                    del need[s]
                    break
        for s in need:
            v, d = need[s]
            eng[q].wait_ge(T.sem[s], v)
            for k, x in clock[d].items():
                if know[q].get(k, 0) < x:
                    know[q][k] = x
        ins = o["fn"]()
        if "remote" in o:
            cnt[o["remote"][0]] = o["remote"][1]
            done[i] = None
            continue
        s = o["sem"] or "s" + q
        inc = o["val"] if o["sem"] else 1
        ins.then_inc(T.sem[s], inc)
        cnt[s] = cnt.get(s, 0) + inc
        done[i] = (s, cnt[s])
        c = dict(know[q])
        c[s] = cnt[s]
        if o["sem"] is None:
            know_self = c
        clock[i] = c
    for s in cnt:
        if know["G"].get(s, 0) < cnt[s]:
            g.wait_ge(T.sem[s], cnt[s])
